import numpy as np
CORES = [19,27,51,107,147,155,179,235,275,283,307,363,403,411,435,491]
N = 16
R, W, B, K = 4096, 64, 256, 2
T = B * K
CAPP = 128
def entries(a): return a.T.reshape(-1)
def pack(v, P): return np.ascontiguousarray(np.asarray(v, np.int32).reshape(-1, P).T)
def lists(rng, how):
    I = rng.integers(0, N * R, (N, T))
    O = np.stack([rng.permutation(np.repeat(np.arange(N), CAPP))[:T] for r in range(N)])
    if how == "full": O = np.stack([rng.permutation(np.repeat(rng.permutation(N)[:T // CAPP], CAPP)) for r in range(N)])
    I = R * O + rng.integers(0, R, (N, T))
    if how == "alike": I = R * O + rng.integers(0, R, (N, 1))
    if how == "edge": I = R * O + np.where(rng.random((N, T)) < 0.5, 0, R - 1)
    if how == "sorted": I = np.sort(I, axis=1)
    return {"idx": np.stack([pack(I[r], 128) for r in range(N)])}
def setup_inputs(rng):
    return dict({"tab": rng.standard_normal((N, R, W), dtype=np.float32)}, **lists(rng, "uniform"))
def setup_inputs_alike(rng):
    d = setup_inputs(rng); d.update(lists(rng, "alike"))
    for k in ("tab",): d[k] = (d[k].astype(np.float32) * 1024.0).astype(d[k].dtype)
    return d
def setup_inputs_edge(rng):
    d = setup_inputs(rng); d.update(lists(rng, "edge"))
    for k in ("tab",): d[k] = (d[k].astype(np.float32) * (1 / 1024.0)).astype(d[k].dtype)
    return d
def setup_inputs_full(rng):
    d = setup_inputs(rng); d.update(lists(rng, "full"))
    return d
def setup_inputs_sorted(rng):
    d = setup_inputs(rng); d.update(lists(rng, "sorted"))
    return d
def check_inputs(x):
    bad = []
    if x["idx"].min() < 0 or x["idx"].max() >= N * R: bad.append("idx out of range")
    if max(int(np.bincount(entries(a) // R, minlength=N).max()) for a in x["idx"]) > CAPP: bad.append("more than CAPP entries of a list point into one rank's part")
    return bad
def reference(tab, idx):
    A = np.concatenate(list(tab), axis=0).astype(np.float64)
    return {"y": np.stack([A[entries(idx[r])].reshape(B, K, W).sum(axis=1) for r in range(N)]).astype(np.float32)}

@@ -1,0 +1,317 @@
+from concourse.bass import DstId, RemoteDMATransfer
+from concourse.mybir import AluOpType, ActivationFunctionType
+
+NCORES = 512
+NPRE = 1
+
+
+def _sb(shape, dtype="float32"):
+    return ("sbuf", shape, dtype)
+
+
+SCRATCH = {
+    "idxs": _sb([128, 4], "int32"),
+    "nat0": _sb([128, 512]), "nat1": _sb([128, 512]), "nat2": _sb([128, 512]), "nat3": _sb([128, 512]),
+    "tabT": _sb([128, 4096]),
+    "ident": _sb([128, 128]), "onesf": _sb([128, 128]), "io128": _sb([128, 128]), "kcode": _sb([128, 128]),
+    "onesb": _sb([128, 128], "bfloat16"), "lstr": _sb([128, 128], "bfloat16"), "cstb": _sb([128, 64], "bfloat16"),
+    "segm": _sb([128, 64]), "e8": _sb([128, 8]), "rsel": _sb([128, 64]),
+    "pidx": _sb([128, 1], "int32"), "p15i": _sb([128, 1], "int32"), "p15f": _sb([128, 1]),
+    "oi8": _sb([128, 8], "int32"), "of8": _sb([128, 8]),
+    "hb": _sb([128, 64], "bfloat16"), "hcum": _sb([128, 64], "bfloat16"),
+    "prod": _sb([128, 64]), "seg": _sb([128, 64]),
+    "sloti": _sb([128, 4], "int32"), "kni": _sb([128, 8], "int32"), "knf": _sb([128, 8]),
+    "amat": _sb([128, 512]), "bmat": _sb([128, 256]),
+    "reqx": _sb([128, 64], "uint16"), "offs": _sb([128, 64], "uint16"),
+    "t16": _sb([128, 4], "int32"), "u15": _sb([128, 4], "int32"), "u15f": _sb([128, 4]),
+    "keyy": _sb([128, 4]), "valn": _sb([128, 4]), "valy": _sb([128, 4]),
+    "aymat": _sb([128, 512]), "bymat": _sb([128, 32]), "offy": _sb([128, 32], "uint16"),
+    "gout": _sb([128, 1024]), "land": _sb([128, 1028]),
+    "gy": _sb([128, 512]), "zz": _sb([128, 256]), "ys": _sb([128, 128]),
+    "pst0": ("psum", [128, 512], "float32"), "pst1": ("psum", [128, 512], "float32"),
+    "pst2": ("psum", [128, 512], "float32"), "pst3": ("psum", [128, 512], "float32"),
+    "psp": ("psum", [128, 512], "float32"), "psr": ("psum", [128, 512], "float32"),
+    "pso0": ("psum", [128, 512], "float32"), "pso1": ("psum", [128, 512], "float32"),
+}
+SEMAPHORES = (["vs", "ps", "acs", "gs", "sidx", "snat0", "snat1", "snat2", "snat3", "rsp", "lsem", "hq", "hr", "hl",
+               "sy0", "sy1"] + ["rq%d" % r for r in range(16)])
+
+_CACHE = {}
+
+
+def _bits(mask):
+    return [i for i in range(16) if (mask >> i) & 1]
+
+
+def _sub(mask, t, e):
+    return sum(1 << i for i in _bits(mask)[t * e:(t + 1) * e])
+
+
+def _plan(T, topo):
+    if "p" in _CACHE:
+        return _CACHE["p"]
+    cores = [int(x) for x in T.cores]
+    groups, relay, serves = {}, {}, {}
+    for s in cores:
+        gr = {"far": [], "cable": [], "rack": [], "same": []}
+        for r, d in enumerate(cores):
+            if d == s:
+                continue
+            if not topo.may_write(s, d):
+                gr["far"].append(r)
+            elif topo.host(d) == topo.host(s):
+                gr["same"].append(r)
+            elif topo.rack(topo.host(d)) == topo.rack(topo.host(s)):
+                gr["rack"].append(r)
+            else:
+                gr["cable"].append(r)
+        groups[s] = gr
+        cand = [x for x in range(NCORES)
+                if T.rank_of(x) is None and topo.chip(x) == topo.chip(s)
+                and topo.rack(topo.host(x)) != topo.rack(topo.host(s)) and topo.may_write(s, x)
+                and all(topo.may_write(x, cores[r]) for r in gr["far"])]
+        cand.sort(key=lambda x: (topo.die(x) == topo.die(s), x))
+        relay[s] = cand[0]
+        serves[cand[0]] = s
+    _CACHE["p"] = {"cores": cores, "groups": groups, "relay": relay, "serves": serves}
+    return _CACHE["p"]
+
+
+def _tr(topo, src_core, dst_core, t, e, sem, src, dst):
+    rid, pid = topo.addr(dst_core, src_core)
+    return RemoteDMATransfer(dst_ids=[DstId(rid=rid, pnc=pid)], dma_engine_mask=_sub(topo.mask(src_core, dst_core), t, e),
+                             remote_sem=sem, src=src, dst=dst)
+
+
+def _share(topo, a, b):
+    return len(_bits(topo.mask(a, b))) // 4
+
+
+def _relay(g, core, s, T, topo, plan):
+    S, cores = T.sem, plan["cores"]
+    sr = T.rank_of(s)
+    far = plan["groups"][s]["far"]
+    nin = len(_bits(topo.mask(s, core)))
+    tot = 0
+    g.wait_ge(S.hq, nin)
+    trs = []
+    for t, d in enumerate(far):
+        e = _share(topo, core, cores[d])
+        trs.append(_tr(topo, core, cores[d], t, e, S["rq%d" % sr], T.reqx[:, 4 * d:4 * d + 4], T.offs[:, 4 * sr:4 * sr + 4]))
+        tot += e
+    g.remote_dma_fused(trs, local_sem=S.hl)
+    g.wait_ge(S.hr, nin)
+    trs = []
+    for t, d in enumerate(far):
+        e = _share(topo, core, cores[d])
+        trs.append(_tr(topo, core, cores[d], t, e, S.rsp, T.gout[:, 64 * d:64 * d + 64], T.land[:, 64 * sr:64 * sr + 64]))
+        tot += e
+    g.remote_dma_fused(trs, local_sem=S.hl)
+    g.wait_ge(S.hl, tot)
+
+
+def rank_program(g, core, T, topo):
+    plan = _plan(T, topo)
+    me = T.rank_of(core)
+    if me is None:
+        s = plan["serves"].get(core)
+        if s is not None:
+            _relay(g, core, s, T, topo, plan)
+        return
+    S, cores = T.sem, plan["cores"]
+    A, AF = AluOpType, ActivationFunctionType
+    v, pe, sc, sy = g.vector, g.tensor, g.scalar, g.sync
+    grp, relay = plan["groups"][core], plan["relay"][core]
+
+    cnt, seen = {}, {}
+    Q = {"v": (v, "vs"), "p": (pe, "ps"), "a": (sc, "acs"), "g": (g, "gs"), "y": (sy, None)}
+
+    def wait(qn, sem, val):
+        if val > 0 and seen.get((qn, sem), 0) < val:
+            seen[(qn, sem)] = val
+            Q[qn][0].wait_ge(S[sem], val)
+
+    def pre(qn, deps=()):
+        own = Q[qn][1]
+        if own is not None:
+            wait(qn, own, cnt.get(own, 0))
+        for sem, val in deps:
+            wait(qn, sem, val)
+
+    def post(qn, ins):
+        own = Q[qn][1]
+        ins.then_inc(S[own], 1)
+        cnt[own] = cnt.get(own, 0) + 1
+        return (own, cnt[own])
+
+    def V(ins_fn, deps=()):
+        pre("v", deps)
+        return post("v", ins_fn())
+
+    def G(ins_fn, deps=()):
+        pre("g", deps)
+        return post("g", ins_fn())
+
+    sy.dma_start(T.idxs[:], T.idx[:]).then_inc(S.sidx, 16)
+    for k in range(4):
+        (sy if k % 2 == 0 else sc).dma_start(T["nat%d" % k][:], T.tab[1024 * k:1024 * (k + 1), :]).then_inc(S["snat%d" % k], 16)
+    t_idx = ("sidx", 16)
+
+    t_onesb = V(lambda: v.memset(T.onesb[:], 1.0))
+    t_onesf = V(lambda: v.memset(T.onesf[:], 1.0))
+    V(lambda: v.memset(T.hcum[:, 0:16], 0.0))
+    V(lambda: v.memset(T.land[:, 1024:1028], 0.0))
+    t_io = G(lambda: g.iota(T.io128[:], [[1, 128]], 0, 0, allow_small_or_imprecise_dtypes=True))
+    t_cst = G(lambda: g.iota(T.cstb[:], [[0, 4], [1, 16]], 0, 0, allow_small_or_imprecise_dtypes=True))
+    t_l = G(lambda: g.affine_select(T.lstr[:], T.onesb[:], [[1, 128]], A.is_ge, 0.0, -1, -1), [t_onesb])
+    t_id = G(lambda: g.affine_select(T.ident[:], T.onesf[:], [[-1, 128]], A.is_equal, 0.0, 0, 1), [t_onesf])
+    t_kc = G(lambda: g.iota(T.kcode[:], [[16, 2], [0, 4], [1, 16]], 0, 0, allow_small_or_imprecise_dtypes=True))
+    G(lambda: g.affine_select(T.e8[:], T.onesf[:, 0:8], [[-16, 8]], A.is_ge, 0.0, 0, 1))
+    t_e8 = G(lambda: g.affine_select(T.e8[:], T.e8[:], [[16, 8]], A.is_ge, 0.0, 15, -1))
+    t_pi = G(lambda: g.iota(T.pidx[:], [[0, 1]], 0, 1))
+    V(lambda: v.tensor_scalar(out=T.segm[:], in0=T.cstb[:], scalar1=1.0, scalar2=None, op0=A.min), [t_cst])
+
+    tT, ev = {}, {}
+
+    def do_T(n):
+        k, u = divmod(n, 4)
+        deps = [("snat%d" % k, 16), t_id] + ([ev[n - 4]] if n >= 4 else [])
+        pre("p", deps)
+        tT[n] = post("p", pe.transpose(T["pst%d" % (n % 4)][:, 0:128], T["nat%d" % k][:, 128 * u:128 * u + 128], T.ident[:]))
+
+    def do_E(n):
+        k, u = divmod(n, 4)
+        qn = "v" if (n >= 8 and n % 2 == 0) else "a"
+        for h in (0, 1):
+            for dup in (0, 1):
+                out = T.tabT[64 * dup:64 * dup + 64, 1024 * k + 2 * u + h:1024 * (k + 1):8]
+                in_ = T["pst%d" % (n % 4)][64 * h:64 * h + 64, 0:128]
+                pre(qn, [tT[n]])
+                ev[n] = post(qn, v.tensor_copy(out, in_) if qn == "v" else sc.activation(out, in_, AF.Copy))
+
+    V(lambda: v.tensor_scalar(out=T.oi8[:, 0:4], in0=T.idxs[:], scalar1=12, scalar2=None, op0=A.logical_shift_right), [t_idx])
+    V(lambda: v.tensor_scalar(out=T.oi8[:, 4:8], in0=T.idxs[:], scalar1=4095, scalar2=None, op0=A.bitwise_and))
+    V(lambda: v.tensor_copy(T.of8[:], T.oi8[:]))
+    for c in range(4):
+        t_h = V(lambda: v.tensor_scalar(out=T.hb[:, 16 * c:16 * c + 16], in0=T.io128[:, 0:16], scalar1=T.of8[:, c:c + 1],
+                                        scalar2=None, op0=A.is_equal), [t_io])
+    V(lambda: v.tensor_scalar(out=T.hcum[:, 16:32], in0=T.io128[:, 0:16], scalar1=T.of8[:, 0:1], scalar2=None, op0=A.is_equal))
+    V(lambda: v.tensor_tensor(out=T.hcum[:, 32:48], in0=T.hb[:, 0:16], in1=T.hb[:, 16:32], op=A.add))
+    t_hc = V(lambda: v.tensor_tensor(out=T.hcum[:, 48:64], in0=T.hcum[:, 32:48], in1=T.hb[:, 32:48], op=A.add))
+    pre("p", [t_onesb, t_cst])
+    pe.matmul(T.psp[:, 0:64], T.onesb[:], T.cstb[:], True, False)
+    pre("p", [t_l, t_h])
+    pe.matmul(T.psp[:, 0:64], T.lstr[:], T.hb[:], False, False)
+    pre("p", [t_hc])
+    t_p = post("p", pe.matmul(T.psp[:, 0:64], T.onesb[:], T.hcum[:], False, True))
+    for n in range(NPRE):
+        do_T(n)
+        do_E(n)
+    V(lambda: v.tensor_tensor(out=T.prod[:], in0=T.psp[:, 0:64], in1=T.hb[:], op=A.mult), [t_p])
+    V(lambda: v.tensor_tensor_scan(T.seg[:], T.segm[:], T.prod[:], 0.0, A.mult, A.add))
+    V(lambda: v.tensor_copy(T.sloti[:], T.seg[:, 15:64:16]))
+    V(lambda: v.tensor_scalar(out=T.kni[:, 0:4], in0=T.sloti[:], scalar1=31, scalar2=None, op0=A.bitwise_and))
+    V(lambda: v.tensor_scalar(out=T.kni[:, 4:8], in0=T.sloti[:], scalar1=5, scalar2=None, op0=A.logical_shift_right))
+    V(lambda: v.tensor_copy(T.knf[:], T.kni[:]))
+    for c in range(4):
+        V(lambda: v.tensor_scalar(out=T.amat[:, 128 * c:128 * c + 128], in0=T.kcode[:], scalar1=T.knf[:, c:c + 1],
+                                  scalar2=None, op0=A.is_equal), [t_kc])
+        t_b = V(lambda: v.tensor_scalar(out=T.bmat[:, 64 * c:64 * c + 64], in0=T.io128[:, 0:64], scalar1=T.knf[:, 4 + c:5 + c],
+                                        scalar2=T.of8[:, 4 + c:5 + c], op0=A.is_equal, op1=A.mult))
+        pre("p", [t_b])
+        ins = pe.matmul(T.psr[:, 0:64], T.amat[:, 128 * c:128 * c + 128], T.bmat[:, 64 * c:64 * c + 64], c == 0, c == 3)
+    t_r = post("p", ins)
+    t_req = V(lambda: v.tensor_copy(T.reqx[:], T.psr[:, 0:64]), [t_r])
+
+    lsem = 0
+    far = grp["far"]
+    pre("g", [t_req])
+    rid, pid = topo.addr(relay, core)
+    mk = topo.mask(core, relay)
+    g.remote_dma(out_ap=T.reqx[:, 4 * far[0]:4 * far[0] + 16], in_ap=T.reqx[:, 4 * far[0]:4 * far[0] + 16], remote_sem=S.hq,
+                 local_sem=S.lsem, pid=pid, routing_id=rid, dma_engine_mask=mk)
+    lsem += len(_bits(mk))
+    for kind in ("cable", "rack", "same"):
+        trs = []
+        for t, d in enumerate(grp[kind]):
+            e = _share(topo, core, cores[d])
+            trs.append(_tr(topo, core, cores[d], t, e, S["rq%d" % me], T.reqx[:, 4 * d:4 * d + 4], T.offs[:, 4 * me:4 * me + 4]))
+            lsem += e
+        g.remote_dma_fused(trs, local_sem=S.lsem)
+
+    V(lambda: v.tensor_scalar(out=T.p15i[:], in0=T.pidx[:], scalar1=15, scalar2=None, op0=A.bitwise_and), [t_pi])
+    V(lambda: v.tensor_copy(T.p15f[:], T.p15i[:]))
+    V(lambda: v.tensor_tensor(out=T.rsel[:], in0=T.ident[:, 0:64], in1=T.ident[:, 64:128], op=A.add), [t_id])
+    V(lambda: v.tensor_scalar(out=T.t16[:], in0=T.sloti[:], scalar1=16, scalar2=None, op0=A.bitwise_and))
+    V(lambda: v.tensor_scalar(out=T.keyy[:], in0=T.t16[:], scalar1=T.p15f[:, 0:1], scalar2=None, op0=A.add))
+    V(lambda: v.tensor_scalar(out=T.u15[:], in0=T.sloti[:], scalar1=15, scalar2=None, op0=A.bitwise_and))
+    V(lambda: v.tensor_copy(T.u15f[:], T.u15[:]))
+    V(lambda: v.tensor_scalar(out=T.valn[:], in0=T.knf[:, 4:8], scalar1=16.0, scalar2=-1024.0, op0=A.mult, op1=A.add))
+    V(lambda: v.tensor_tensor(out=T.valy[:], in0=T.valn[:], in1=T.u15f[:], op=A.add))
+    for c in range(4):
+        V(lambda: v.tensor_scalar(out=T.aymat[:, 128 * c:128 * c + 128], in0=T.kcode[:], scalar1=T.keyy[:, c:c + 1],
+                                  scalar2=None, op0=A.is_equal))
+        t_by = V(lambda: v.tensor_scalar(out=T.bymat[:, 8 * c:8 * c + 8], in0=T.e8[:], scalar1=T.valy[:, c:c + 1],
+                                         scalar2=None, op0=A.mult), [t_e8])
+
+    for n in range(NPRE, 16):
+        do_T(n)
+        do_E(n)
+    t_tab = [ev[15], ev[14]]
+    for c in range(4):
+        pre("p", [t_by])
+        t_py = post("p", pe.matmul(T.psr[:, 64 + 8 * c:72 + 8 * c], T.aymat[:, 128 * c:128 * c + 128], T.bymat[:, 8 * c:8 * c + 8],
+                                   True, True))
+
+    win = T.tabT[:, 0:4096]
+    nrq = {}
+    for r, d in enumerate(cores):
+        if r != me:
+            src = plan["relay"][d] if me in plan["groups"][d]["far"] else d
+            nrq[r] = _share(topo, src, core)
+    for kind in ("cable", "rack", "far", "same"):
+        rs = grp[kind]
+        deps = t_tab + [("rq%d" % r, nrq[r]) for r in rs]
+        if kind == "same":
+            for r in rs:
+                t_g = V(lambda: v.tensor_copy(T.gout[:, 64 * r:64 * r + 64], win.indirect(T.offs[:, 4 * r:4 * r + 4])), deps)
+        else:
+            r0 = rs[0]
+            t_g = V(lambda: v.tensor_copy(T.gout[:, 64 * r0:64 * r0 + 256], win.indirect(T.offs[:, 4 * r0:4 * r0 + 16])), deps)
+        pre("g", [t_g])
+        if kind == "far":
+            g.remote_dma(out_ap=T.gout[:, 64 * r0:64 * r0 + 256], in_ap=T.gout[:, 64 * r0:64 * r0 + 256], remote_sem=S.hr,
+                         local_sem=S.lsem, pid=pid, routing_id=rid, dma_engine_mask=mk)
+            lsem += len(_bits(mk))
+        else:
+            trs = []
+            for t, d in enumerate(rs):
+                e = _share(topo, core, cores[d])
+                trs.append(_tr(topo, core, cores[d], t, e, S.rsp, T.gout[:, 64 * d:64 * d + 64], T.land[:, 64 * me:64 * me + 64]))
+                lsem += e
+            g.remote_dma_fused(trs, local_sem=S.lsem)
+    V(lambda: v.tensor_copy(T.land[:, 64 * me:64 * me + 64], win.indirect(T.reqx[:, 4 * me:4 * me + 4])))
+    t_oy = V(lambda: v.tensor_scalar(out=T.offy[:], in0=T.psr[:, 64:96], scalar1=1024.0, scalar2=None, op0=A.add), [t_py])
+
+    t_rsp = ("rsp", sum(nrq.values()))
+    lwin = T.land[:, 0:1028]
+    t_g0 = V(lambda: v.tensor_copy(T.gy[:, 0:256], lwin.indirect(T.offy[:, 0:16])), [t_rsp])
+    pre("a", [t_rsp, t_oy])
+    t_g1 = post("a", sc.activation(T.gy[:, 256:512], lwin.indirect(T.offy[:, 16:32]), AF.Copy))
+    t_z0 = V(lambda: v.tensor_tensor(out=T.zz[:, 0:128], in0=T.gy[:, 0:256:2], in1=T.gy[:, 1:256:2], op=A.add))
+    pre("p", [t_z0])
+    t_m0 = post("p", pe.matmul(T.pso0[:, 0:64], T.zz[:, 0:128], T.rsel[:], True, True))
+    t_z1 = V(lambda: v.tensor_tensor(out=T.zz[:, 128:256], in0=T.gy[:, 256:512:2], in1=T.gy[:, 257:512:2], op=A.add), [t_g1])
+    pre("p", [t_z1])
+    t_m1 = post("p", pe.matmul(T.pso1[:, 0:64], T.zz[:, 128:256], T.rsel[:], True, True))
+    pre("a", [t_m0])
+    post("a", sc.activation(T.ys[:, 0:64], T.pso0[:, 0:64], AF.Copy))
+    pre("a")
+    sc.dma_start(T.y[0:128, :], T.ys[:, 0:64]).then_inc(S.sy0, 16)
+    t_y1 = V(lambda: v.tensor_copy(T.ys[:, 64:128], T.pso1[:, 0:64]), [t_m1])
+    pre("y", [t_y1])
+    sy.dma_start(T.y[128:256, :], T.ys[:, 64:128]).then_inc(S.sy1, 16)
+
+    fin = [(k, n) for k, n in cnt.items()] + [t_idx, t_rsp, ("lsem", lsem), ("sy0", 16), ("sy1", 16)]
+    fin += [("snat%d" % k, 16) for k in range(4)] + [("rq%d" % r, n) for r, n in nrq.items()]
+    pre("g", fin)

@@ -3,6 +3,7 @@ from concourse.mybir import AluOpType, ActivationFunctionType
 
 NCORES = 512
 NPRE = 1
+NSTAGE = 64
 
 
 def _sb(shape, dtype="float32"):
@@ -15,10 +16,10 @@ SCRATCH = {
     "tabT": _sb([128, 4096]),
     "ident": _sb([128, 128]), "onesf": _sb([128, 128]), "io128": _sb([128, 128]), "kcode": _sb([128, 128]),
     "onesb": _sb([128, 128], "bfloat16"), "lstr": _sb([128, 128], "bfloat16"), "cstb": _sb([128, 64], "bfloat16"),
-    "segm": _sb([128, 64]), "e8": _sb([128, 8]), "rsel": _sb([128, 64]),
+    "segm": _sb([128, 64]), "e8a": _sb([128, 8]), "e8": _sb([128, 8]), "rsel": _sb([128, 64]),
     "pidx": _sb([128, 1], "int32"), "p15i": _sb([128, 1], "int32"), "p15f": _sb([128, 1]),
     "oi8": _sb([128, 8], "int32"), "of8": _sb([128, 8]),
-    "hb": _sb([128, 64], "bfloat16"), "hcum": _sb([128, 64], "bfloat16"),
+    "hb": _sb([128, 64], "bfloat16"), "hcum": _sb([128, 192], "bfloat16"),
     "prod": _sb([128, 64]), "seg": _sb([128, 64]),
     "sloti": _sb([128, 4], "int32"), "kni": _sb([128, 8], "int32"), "knf": _sb([128, 8]),
     "amat": _sb([128, 512]), "bmat": _sb([128, 256]),
@@ -33,8 +34,8 @@ SCRATCH = {
     "psp": ("psum", [128, 512], "float32"), "psr": ("psum", [128, 512], "float32"),
     "pso0": ("psum", [128, 512], "float32"), "pso1": ("psum", [128, 512], "float32"),
 }
-SEMAPHORES = (["vs", "ps", "acs", "gs", "sidx", "snat0", "snat1", "snat2", "snat3", "rsp", "lsem", "hq", "hr", "hl",
-               "sy0", "sy1"] + ["rq%d" % r for r in range(16)])
+SEMAPHORES = (["sidx", "snat0", "snat1", "snat2", "snat3", "rsp", "lsem", "hq", "hr", "hl", "sy0", "sy1"]
+              + ["rq%d" % r for r in range(16)] + ["x%d" % i for i in range(NSTAGE)])
 
 _CACHE = {}
 
@@ -71,8 +72,9 @@ def _plan(T, topo):
                 and topo.rack(topo.host(x)) != topo.rack(topo.host(s)) and topo.may_write(s, x)
                 and all(topo.may_write(x, cores[r]) for r in gr["far"])]
         cand.sort(key=lambda x: (topo.die(x) == topo.die(s), x))
-        relay[s] = cand[0]
-        serves[cand[0]] = s
+        relay[s] = cand[0:2]
+        for i, x in enumerate(relay[s]):
+            serves[x] = (s, i)
     _CACHE["p"] = {"cores": cores, "groups": groups, "relay": relay, "serves": serves}
     return _CACHE["p"]
 
@@ -83,30 +85,24 @@ def _tr(topo, src_core, dst_core, t, e, sem, src, dst):
                              remote_sem=sem, src=src, dst=dst)
 
 
-def _share(topo, a, b):
-    return len(_bits(topo.mask(a, b))) // 4
+def _share(topo, a, b, n=4):
+    return len(_bits(topo.mask(a, b))) // n
 
 
-def _relay(g, core, s, T, topo, plan):
+def _relay(g, core, s, half, T, topo, plan):
     S, cores = T.sem, plan["cores"]
     sr = T.rank_of(s)
-    far = plan["groups"][s]["far"]
-    nin = len(_bits(topo.mask(s, core)))
+    far = plan["groups"][s]["far"][2 * half:2 * half + 2]
+    nin = _share(topo, s, core, 2)
     tot = 0
-    g.wait_ge(S.hq, nin)
-    trs = []
-    for t, d in enumerate(far):
-        e = _share(topo, core, cores[d])
-        trs.append(_tr(topo, core, cores[d], t, e, S["rq%d" % sr], T.reqx[:, 4 * d:4 * d + 4], T.offs[:, 4 * sr:4 * sr + 4]))
-        tot += e
-    g.remote_dma_fused(trs, local_sem=S.hl)
-    g.wait_ge(S.hr, nin)
-    trs = []
-    for t, d in enumerate(far):
-        e = _share(topo, core, cores[d])
-        trs.append(_tr(topo, core, cores[d], t, e, S.rsp, T.gout[:, 64 * d:64 * d + 64], T.land[:, 64 * sr:64 * sr + 64]))
-        tot += e
-    g.remote_dma_fused(trs, local_sem=S.hl)
+    for sem_in, sem_out, buf, land, w in ((S.hq, S["rq%d" % sr], T.reqx, T.offs, 4), (S.hr, S.rsp, T.gout, T.land, 64)):
+        g.wait_ge(sem_in, nin)
+        trs = []
+        for t, d in enumerate(far):
+            e = _share(topo, core, cores[d], 2)
+            trs.append(_tr(topo, core, cores[d], t, e, sem_out, buf[:, w * d:w * d + w], land[:, w * sr:w * sr + w]))
+            tot += e
+        g.remote_dma_fused(trs, local_sem=S.hl)
     g.wait_ge(S.hl, tot)
 
 
@@ -116,68 +112,61 @@ def rank_program(g, core, T, topo):
     if me is None:
         s = plan["serves"].get(core)
         if s is not None:
-            _relay(g, core, s, T, topo, plan)
+            _relay(g, core, s[0], s[1], T, topo, plan)
         return
     S, cores = T.sem, plan["cores"]
     A, AF = AluOpType, ActivationFunctionType
     v, pe, sc, sy = g.vector, g.tensor, g.scalar, g.sync
     grp, relay = plan["groups"][core], plan["relay"][core]
+    Q = {"v": v, "p": pe, "a": sc, "g": g, "y": sy}
+    seen, nx = {}, [0]
 
-    cnt, seen = {}, {}
-    Q = {"v": (v, "vs"), "p": (pe, "ps"), "a": (sc, "acs"), "g": (g, "gs"), "y": (sy, None)}
+    def stage():
+        nx[0] += 1
+        return ["x%d" % (nx[0] - 1), 0]
 
-    def wait(qn, sem, val):
-        if val > 0 and seen.get((qn, sem), 0) < val:
-            seen[(qn, sem)] = val
-            Q[qn][0].wait_ge(S[sem], val)
+    def emit(qn, fn, deps=(), st=None):
+        for d in deps:
+            if d[1] > 0 and seen.get((qn, d[0]), 0) < d[1]:
+                seen[(qn, d[0])] = d[1]
+                Q[qn].wait_ge(S[d[0]], d[1])
+        ins = fn()
+        if st is not None:
+            ins.then_inc(S[st[0]], 1)
+            st[1] += 1
+        return st
 
-    def pre(qn, deps=()):
-        own = Q[qn][1]
-        if own is not None:
-            wait(qn, own, cnt.get(own, 0))
-        for sem, val in deps:
-            wait(qn, sem, val)
-
-    def post(qn, ins):
-        own = Q[qn][1]
-        ins.then_inc(S[own], 1)
-        cnt[own] = cnt.get(own, 0) + 1
-        return (own, cnt[own])
-
-    def V(ins_fn, deps=()):
-        pre("v", deps)
-        return post("v", ins_fn())
-
-    def G(ins_fn, deps=()):
-        pre("g", deps)
-        return post("g", ins_fn())
+    def one(qn, fn, deps=()):
+        return emit(qn, fn, deps, stage())
 
     sy.dma_start(T.idxs[:], T.idx[:]).then_inc(S.sidx, 16)
     for k in range(4):
         (sy if k % 2 == 0 else sc).dma_start(T["nat%d" % k][:], T.tab[1024 * k:1024 * (k + 1), :]).then_inc(S["snat%d" % k], 16)
     t_idx = ("sidx", 16)
 
-    t_onesb = V(lambda: v.memset(T.onesb[:], 1.0))
-    t_onesf = V(lambda: v.memset(T.onesf[:], 1.0))
-    V(lambda: v.memset(T.hcum[:, 0:16], 0.0))
-    V(lambda: v.memset(T.land[:, 1024:1028], 0.0))
-    t_io = G(lambda: g.iota(T.io128[:], [[1, 128]], 0, 0, allow_small_or_imprecise_dtypes=True))
-    t_cst = G(lambda: g.iota(T.cstb[:], [[0, 4], [1, 16]], 0, 0, allow_small_or_imprecise_dtypes=True))
-    t_l = G(lambda: g.affine_select(T.lstr[:], T.onesb[:], [[1, 128]], A.is_ge, 0.0, -1, -1), [t_onesb])
-    t_id = G(lambda: g.affine_select(T.ident[:], T.onesf[:], [[-1, 128]], A.is_equal, 0.0, 0, 1), [t_onesf])
-    t_kc = G(lambda: g.iota(T.kcode[:], [[16, 2], [0, 4], [1, 16]], 0, 0, allow_small_or_imprecise_dtypes=True))
-    G(lambda: g.affine_select(T.e8[:], T.onesf[:, 0:8], [[-16, 8]], A.is_ge, 0.0, 0, 1))
-    t_e8 = G(lambda: g.affine_select(T.e8[:], T.e8[:], [[16, 8]], A.is_ge, 0.0, 15, -1))
-    t_pi = G(lambda: g.iota(T.pidx[:], [[0, 1]], 0, 1))
-    V(lambda: v.tensor_scalar(out=T.segm[:], in0=T.cstb[:], scalar1=1.0, scalar2=None, op0=A.min), [t_cst])
+    t_ob = one("v", lambda: v.memset(T.onesb[:], 1.0))
+    t_of = one("v", lambda: v.memset(T.onesf[:], 1.0))
+    t_hz = stage()
+    for a, b in ((0, 16), (64, 96), (128, 176)):
+        emit("v", lambda: v.memset(T.hcum[:, a:b], 0.0), (), t_hz)
+    t_lz = one("v", lambda: v.memset(T.land[:, 1024:1028], 0.0))
+    t_io = one("g", lambda: g.iota(T.io128[:], [[1, 128]], 0, 0, allow_small_or_imprecise_dtypes=True))
+    t_cst = one("g", lambda: g.iota(T.cstb[:], [[0, 4], [1, 16]], 0, 0, allow_small_or_imprecise_dtypes=True))
+    t_l = one("g", lambda: g.affine_select(T.lstr[:], T.onesb[:], [[1, 128]], A.is_ge, 0.0, -1, -1), [t_ob])
+    t_id = one("g", lambda: g.affine_select(T.ident[:], T.onesf[:], [[-1, 128]], A.is_equal, 0.0, 0, 1), [t_of])
+    t_kc = one("g", lambda: g.iota(T.kcode[:], [[16, 2], [0, 4], [1, 16]], 0, 0, allow_small_or_imprecise_dtypes=True))
+    t_e8a = one("g", lambda: g.affine_select(T.e8a[:], T.onesf[:, 0:8], [[-16, 8]], A.is_ge, 0.0, 0, 1))
+    t_e8 = one("g", lambda: g.affine_select(T.e8[:], T.e8a[:], [[16, 8]], A.is_ge, 0.0, 15, -1), [t_e8a])
+    t_pi = one("g", lambda: g.iota(T.pidx[:], [[0, 1]], 0, 1))
+    t_sg = one("v", lambda: v.tensor_scalar(out=T.segm[:], in0=T.cstb[:], scalar1=1.0, scalar2=None, op0=A.min), [t_cst])
 
-    tT, ev = {}, {}
+    tb = [stage() for b in range(4)]
+    evb = [stage() for b in range(4)]
 
     def do_T(n):
         k, u = divmod(n, 4)
-        deps = [("snat%d" % k, 16), t_id] + ([ev[n - 4]] if n >= 4 else [])
-        pre("p", deps)
-        tT[n] = post("p", pe.transpose(T["pst%d" % (n % 4)][:, 0:128], T["nat%d" % k][:, 128 * u:128 * u + 128], T.ident[:]))
+        emit("p", lambda: pe.transpose(T["pst%d" % (n % 4)][:, 0:128], T["nat%d" % k][:, 128 * u:128 * u + 128], T.ident[:]),
+             [("snat%d" % k, 16), t_id, evb[n % 4]], tb[n % 4])
 
     def do_E(n):
         k, u = divmod(n, 4)
@@ -186,132 +175,136 @@ def rank_program(g, core, T, topo):
             for dup in (0, 1):
                 out = T.tabT[64 * dup:64 * dup + 64, 1024 * k + 2 * u + h:1024 * (k + 1):8]
                 in_ = T["pst%d" % (n % 4)][64 * h:64 * h + 64, 0:128]
-                pre(qn, [tT[n]])
-                ev[n] = post(qn, v.tensor_copy(out, in_) if qn == "v" else sc.activation(out, in_, AF.Copy))
+                emit(qn, lambda: v.tensor_copy(out, in_) if qn == "v" else sc.activation(out, in_, AF.Copy),
+                     [tb[n % 4]], evb[n % 4])
 
-    V(lambda: v.tensor_scalar(out=T.oi8[:, 0:4], in0=T.idxs[:], scalar1=12, scalar2=None, op0=A.logical_shift_right), [t_idx])
-    V(lambda: v.tensor_scalar(out=T.oi8[:, 4:8], in0=T.idxs[:], scalar1=4095, scalar2=None, op0=A.bitwise_and))
-    V(lambda: v.tensor_copy(T.of8[:], T.oi8[:]))
+    s1 = stage()
+    emit("v", lambda: v.tensor_scalar(out=T.oi8[:, 0:4], in0=T.idxs[:], scalar1=12, scalar2=None, op0=A.logical_shift_right),
+         [t_idx], s1)
+    emit("v", lambda: v.tensor_scalar(out=T.oi8[:, 4:8], in0=T.idxs[:], scalar1=4095, scalar2=None, op0=A.bitwise_and), (), s1)
+    s2 = one("v", lambda: v.tensor_copy(T.of8[:], T.oi8[:]), [s1])
+    s3, s4 = stage(), stage()
     for c in range(4):
-        t_h = V(lambda: v.tensor_scalar(out=T.hb[:, 16 * c:16 * c + 16], in0=T.io128[:, 0:16], scalar1=T.of8[:, c:c + 1],
-                                        scalar2=None, op0=A.is_equal), [t_io])
-    V(lambda: v.tensor_scalar(out=T.hcum[:, 16:32], in0=T.io128[:, 0:16], scalar1=T.of8[:, 0:1], scalar2=None, op0=A.is_equal))
-    V(lambda: v.tensor_tensor(out=T.hcum[:, 32:48], in0=T.hb[:, 0:16], in1=T.hb[:, 16:32], op=A.add))
-    t_hc = V(lambda: v.tensor_tensor(out=T.hcum[:, 48:64], in0=T.hcum[:, 32:48], in1=T.hb[:, 32:48], op=A.add))
-    pre("p", [t_onesb, t_cst])
-    pe.matmul(T.psp[:, 0:64], T.onesb[:], T.cstb[:], True, False)
-    pre("p", [t_l, t_h])
-    pe.matmul(T.psp[:, 0:64], T.lstr[:], T.hb[:], False, False)
-    pre("p", [t_hc])
-    t_p = post("p", pe.matmul(T.psp[:, 0:64], T.onesb[:], T.hcum[:], False, True))
+        emit("v", lambda: v.tensor_scalar(out=T.hb[:, 16 * c:16 * c + 16], in0=T.io128[:, 0:16], scalar1=T.of8[:, c:c + 1],
+                                          scalar2=None, op0=A.is_equal), [s2, t_io], s3)
+    for c in range(3):
+        emit("v", lambda: v.tensor_scalar(out=T.hcum[:, 64 * c + 16 * (c + 1):64 * c + 64], in0=T.cstb[:, 0:48 - 16 * c],
+                                          scalar1=T.of8[:, c:c + 1], scalar2=None, op0=A.is_equal), [t_cst], s4)
+    emit("p", lambda: pe.matmul(T.psp[:, 0:64], T.onesb[:], T.cstb[:], True, False), [t_ob, t_cst])
+    emit("p", lambda: pe.matmul(T.psp[:, 0:64], T.lstr[:], T.hb[:], False, False), [t_l, s3])
+    s5 = stage()
+    for c in range(3):
+        emit("p", lambda: pe.matmul(T.psp[:, 0:64], T.onesb[:], T.hcum[:, 64 * c:64 * c + 64], False, c == 2), [s4, t_hz],
+             s5 if c == 2 else None)
     for n in range(NPRE):
         do_T(n)
         do_E(n)
-    V(lambda: v.tensor_tensor(out=T.prod[:], in0=T.psp[:, 0:64], in1=T.hb[:], op=A.mult), [t_p])
-    V(lambda: v.tensor_tensor_scan(T.seg[:], T.segm[:], T.prod[:], 0.0, A.mult, A.add))
-    V(lambda: v.tensor_copy(T.sloti[:], T.seg[:, 15:64:16]))
-    V(lambda: v.tensor_scalar(out=T.kni[:, 0:4], in0=T.sloti[:], scalar1=31, scalar2=None, op0=A.bitwise_and))
-    V(lambda: v.tensor_scalar(out=T.kni[:, 4:8], in0=T.sloti[:], scalar1=5, scalar2=None, op0=A.logical_shift_right))
-    V(lambda: v.tensor_copy(T.knf[:], T.kni[:]))
+    s6 = one("v", lambda: v.tensor_tensor(out=T.prod[:], in0=T.psp[:, 0:64], in1=T.hb[:], op=A.mult), [s5, s3])
+    s7 = one("v", lambda: v.tensor_tensor_scan(T.seg[:], T.segm[:], T.prod[:], 0.0, A.mult, A.add), [s6, t_sg])
+    s8 = one("v", lambda: v.tensor_copy(T.sloti[:], T.seg[:, 15:64:16]), [s7])
+    s9 = stage()
+    emit("v", lambda: v.tensor_scalar(out=T.kni[:, 0:4], in0=T.sloti[:], scalar1=31, scalar2=None, op0=A.bitwise_and), [s8], s9)
+    emit("v", lambda: v.tensor_scalar(out=T.kni[:, 4:8], in0=T.sloti[:], scalar1=5, scalar2=None, op0=A.logical_shift_right),
+         (), s9)
+    s10 = one("v", lambda: v.tensor_copy(T.knf[:], T.kni[:]), [s9])
+    s12 = stage()
     for c in range(4):
-        V(lambda: v.tensor_scalar(out=T.amat[:, 128 * c:128 * c + 128], in0=T.kcode[:], scalar1=T.knf[:, c:c + 1],
-                                  scalar2=None, op0=A.is_equal), [t_kc])
-        t_b = V(lambda: v.tensor_scalar(out=T.bmat[:, 64 * c:64 * c + 64], in0=T.io128[:, 0:64], scalar1=T.knf[:, 4 + c:5 + c],
-                                        scalar2=T.of8[:, 4 + c:5 + c], op0=A.is_equal, op1=A.mult))
-        pre("p", [t_b])
-        ins = pe.matmul(T.psr[:, 0:64], T.amat[:, 128 * c:128 * c + 128], T.bmat[:, 64 * c:64 * c + 64], c == 0, c == 3)
-    t_r = post("p", ins)
-    t_req = V(lambda: v.tensor_copy(T.reqx[:], T.psr[:, 0:64]), [t_r])
+        s11 = stage()
+        emit("v", lambda: v.tensor_scalar(out=T.amat[:, 128 * c:128 * c + 128], in0=T.kcode[:], scalar1=T.knf[:, c:c + 1],
+                                          scalar2=None, op0=A.is_equal), [s10, t_kc], s11)
+        emit("v", lambda: v.tensor_scalar(out=T.bmat[:, 64 * c:64 * c + 64], in0=T.io128[:, 0:64], scalar1=T.knf[:, 4 + c:5 + c],
+                                          scalar2=T.of8[:, 4 + c:5 + c], op0=A.is_equal, op1=A.mult), (), s11)
+        emit("p", lambda: pe.matmul(T.psr[:, 0:64], T.amat[:, 128 * c:128 * c + 128], T.bmat[:, 64 * c:64 * c + 64],
+                                    c == 0, c == 3), [s11], s12 if c == 3 else None)
+    t_req = one("v", lambda: v.tensor_copy(T.reqx[:], T.psr[:, 0:64]), [s12])
 
-    lsem = 0
+    lsem = [0]
     far = grp["far"]
-    pre("g", [t_req])
-    rid, pid = topo.addr(relay, core)
-    mk = topo.mask(core, relay)
-    g.remote_dma(out_ap=T.reqx[:, 4 * far[0]:4 * far[0] + 16], in_ap=T.reqx[:, 4 * far[0]:4 * far[0] + 16], remote_sem=S.hq,
-                 local_sem=S.lsem, pid=pid, routing_id=rid, dma_engine_mask=mk)
-    lsem += len(_bits(mk))
-    for kind in ("cable", "rack", "same"):
-        trs = []
-        for t, d in enumerate(grp[kind]):
-            e = _share(topo, core, cores[d])
-            trs.append(_tr(topo, core, cores[d], t, e, S["rq%d" % me], T.reqx[:, 4 * d:4 * d + 4], T.offs[:, 4 * me:4 * me + 4]))
-            lsem += e
-        g.remote_dma_fused(trs, local_sem=S.lsem)
 
-    V(lambda: v.tensor_scalar(out=T.p15i[:], in0=T.pidx[:], scalar1=15, scalar2=None, op0=A.bitwise_and), [t_pi])
-    V(lambda: v.tensor_copy(T.p15f[:], T.p15i[:]))
-    V(lambda: v.tensor_tensor(out=T.rsel[:], in0=T.ident[:, 0:64], in1=T.ident[:, 64:128], op=A.add), [t_id])
-    V(lambda: v.tensor_scalar(out=T.t16[:], in0=T.sloti[:], scalar1=16, scalar2=None, op0=A.bitwise_and))
-    V(lambda: v.tensor_scalar(out=T.keyy[:], in0=T.t16[:], scalar1=T.p15f[:, 0:1], scalar2=None, op0=A.add))
-    V(lambda: v.tensor_scalar(out=T.u15[:], in0=T.sloti[:], scalar1=15, scalar2=None, op0=A.bitwise_and))
-    V(lambda: v.tensor_copy(T.u15f[:], T.u15[:]))
-    V(lambda: v.tensor_scalar(out=T.valn[:], in0=T.knf[:, 4:8], scalar1=16.0, scalar2=-1024.0, op0=A.mult, op1=A.add))
-    V(lambda: v.tensor_tensor(out=T.valy[:], in0=T.valn[:], in1=T.u15f[:], op=A.add))
+    def to_relays(buf, w, sem):
+        trs = []
+        for i, x in enumerate(relay):
+            e = _share(topo, core, x, 2)
+            ap = buf[:, w * far[2 * i]:w * far[2 * i] + 2 * w]
+            trs.append(_tr(topo, core, x, i, e, sem, ap, ap))
+            lsem[0] += e
+        return g.remote_dma_fused(trs, local_sem=S.lsem)
+
+    def fan(rs, sem, buf, w, dst):
+        trs = []
+        for t, d in enumerate(rs):
+            e = _share(topo, core, cores[d])
+            trs.append(_tr(topo, core, cores[d], t, e, sem, buf[:, w * d:w * d + w], dst))
+            lsem[0] += e
+        return g.remote_dma_fused(trs, local_sem=S.lsem)
+
+    emit("g", lambda: to_relays(T.reqx, 4, S.hq), [t_req])
+    for kind in ("cable", "rack", "same"):
+        fan(grp[kind], S["rq%d" % me], T.reqx, 4, T.offs[:, 4 * me:4 * me + 4])
+
+    y1 = one("v", lambda: v.tensor_scalar(out=T.p15i[:], in0=T.pidx[:], scalar1=15, scalar2=None, op0=A.bitwise_and), [t_pi])
+    y4 = stage()
+    emit("v", lambda: v.tensor_scalar(out=T.t16[:], in0=T.sloti[:], scalar1=16, scalar2=None, op0=A.bitwise_and), (), y4)
+    emit("v", lambda: v.tensor_scalar(out=T.u15[:], in0=T.sloti[:], scalar1=15, scalar2=None, op0=A.bitwise_and), (), y4)
+    y3 = one("v", lambda: v.tensor_tensor(out=T.rsel[:], in0=T.ident[:, 0:64], in1=T.ident[:, 64:128], op=A.add), [t_id])
+    y2 = one("v", lambda: v.tensor_copy(T.p15f[:], T.p15i[:]), [y1])
+    y5 = stage()
+    emit("v", lambda: v.tensor_scalar(out=T.keyy[:], in0=T.t16[:], scalar1=T.p15f[:, 0:1], scalar2=None, op0=A.add), [y4, y2], y5)
+    emit("v", lambda: v.tensor_copy(T.u15f[:], T.u15[:]), (), y5)
+    emit("v", lambda: v.tensor_scalar(out=T.valn[:], in0=T.knf[:, 4:8], scalar1=16.0, scalar2=-1024.0, op0=A.mult, op1=A.add),
+         (), y5)
+    y6 = one("v", lambda: v.tensor_tensor(out=T.valy[:], in0=T.valn[:], in1=T.u15f[:], op=A.add), [y5])
+    y7 = stage()
     for c in range(4):
-        V(lambda: v.tensor_scalar(out=T.aymat[:, 128 * c:128 * c + 128], in0=T.kcode[:], scalar1=T.keyy[:, c:c + 1],
-                                  scalar2=None, op0=A.is_equal))
-        t_by = V(lambda: v.tensor_scalar(out=T.bymat[:, 8 * c:8 * c + 8], in0=T.e8[:], scalar1=T.valy[:, c:c + 1],
-                                         scalar2=None, op0=A.mult), [t_e8])
+        emit("v", lambda: v.tensor_scalar(out=T.aymat[:, 128 * c:128 * c + 128], in0=T.kcode[:], scalar1=T.keyy[:, c:c + 1],
+                                          scalar2=None, op0=A.is_equal), (), y7)
+        emit("v", lambda: v.tensor_scalar(out=T.bymat[:, 8 * c:8 * c + 8], in0=T.e8[:], scalar1=T.valy[:, c:c + 1],
+                                          scalar2=None, op0=A.mult), [y6, t_e8], y7)
 
     for n in range(NPRE, 16):
         do_T(n)
         do_E(n)
-    t_tab = [ev[15], ev[14]]
+    y8 = stage()
     for c in range(4):
-        pre("p", [t_by])
-        t_py = post("p", pe.matmul(T.psr[:, 64 + 8 * c:72 + 8 * c], T.aymat[:, 128 * c:128 * c + 128], T.bymat[:, 8 * c:8 * c + 8],
-                                   True, True))
+        emit("p", lambda: pe.matmul(T.psr[:, 64 + 8 * c:72 + 8 * c], T.aymat[:, 128 * c:128 * c + 128],
+                                    T.bymat[:, 8 * c:8 * c + 8], True, True), [y7, t_req], y8)
 
     win = T.tabT[:, 0:4096]
     nrq = {}
     for r, d in enumerate(cores):
         if r != me:
-            src = plan["relay"][d] if me in plan["groups"][d]["far"] else d
-            nrq[r] = _share(topo, src, core)
-    for kind in ("cable", "rack", "far", "same"):
+            isfar = me in plan["groups"][d]["far"]
+            nrq[r] = _share(topo, plan["relay"][d][0], core, 2) if isfar else _share(topo, d, core)
+    for kind in ("cable", "far", "rack", "same"):
         rs = grp[kind]
-        deps = t_tab + [("rq%d" % r, nrq[r]) for r in rs]
+        deps = evb + [("rq%d" % r, nrq[r]) for r in rs]
+        t_g = stage()
         if kind == "same":
             for r in rs:
-                t_g = V(lambda: v.tensor_copy(T.gout[:, 64 * r:64 * r + 64], win.indirect(T.offs[:, 4 * r:4 * r + 4])), deps)
+                emit("v", lambda: v.tensor_copy(T.gout[:, 64 * r:64 * r + 64], win.indirect(T.offs[:, 4 * r:4 * r + 4])), deps, t_g)
         else:
             r0 = rs[0]
-            t_g = V(lambda: v.tensor_copy(T.gout[:, 64 * r0:64 * r0 + 256], win.indirect(T.offs[:, 4 * r0:4 * r0 + 16])), deps)
-        pre("g", [t_g])
+            emit("v", lambda: v.tensor_copy(T.gout[:, 64 * r0:64 * r0 + 256], win.indirect(T.offs[:, 4 * r0:4 * r0 + 16])),
+                 deps, t_g)
         if kind == "far":
-            g.remote_dma(out_ap=T.gout[:, 64 * r0:64 * r0 + 256], in_ap=T.gout[:, 64 * r0:64 * r0 + 256], remote_sem=S.hr,
-                         local_sem=S.lsem, pid=pid, routing_id=rid, dma_engine_mask=mk)
-            lsem += len(_bits(mk))
+            emit("g", lambda: to_relays(T.gout, 64, S.hr), [t_g])
         else:
-            trs = []
-            for t, d in enumerate(rs):
-                e = _share(topo, core, cores[d])
-                trs.append(_tr(topo, core, cores[d], t, e, S.rsp, T.gout[:, 64 * d:64 * d + 64], T.land[:, 64 * me:64 * me + 64]))
-                lsem += e
-            g.remote_dma_fused(trs, local_sem=S.lsem)
-    V(lambda: v.tensor_copy(T.land[:, 64 * me:64 * me + 64], win.indirect(T.reqx[:, 4 * me:4 * me + 4])))
-    t_oy = V(lambda: v.tensor_scalar(out=T.offy[:], in0=T.psr[:, 64:96], scalar1=1024.0, scalar2=None, op0=A.add), [t_py])
+            emit("g", lambda: fan(rs, S.rsp, T.gout, 64, T.land[:, 64 * me:64 * me + 64]), [t_g])
+    t_own = one("v", lambda: v.tensor_copy(T.land[:, 64 * me:64 * me + 64], win.indirect(T.reqx[:, 4 * me:4 * me + 4])), [t_req])
+    t_oy = one("v", lambda: v.tensor_scalar(out=T.offy[:], in0=T.psr[:, 64:96], scalar1=1024.0, scalar2=None, op0=A.add), [y8])
 
     t_rsp = ("rsp", sum(nrq.values()))
     lwin = T.land[:, 0:1028]
-    t_g0 = V(lambda: v.tensor_copy(T.gy[:, 0:256], lwin.indirect(T.offy[:, 0:16])), [t_rsp])
-    pre("a", [t_rsp, t_oy])
-    t_g1 = post("a", sc.activation(T.gy[:, 256:512], lwin.indirect(T.offy[:, 16:32]), AF.Copy))
-    t_z0 = V(lambda: v.tensor_tensor(out=T.zz[:, 0:128], in0=T.gy[:, 0:256:2], in1=T.gy[:, 1:256:2], op=A.add))
-    pre("p", [t_z0])
-    t_m0 = post("p", pe.matmul(T.pso0[:, 0:64], T.zz[:, 0:128], T.rsel[:], True, True))
-    t_z1 = V(lambda: v.tensor_tensor(out=T.zz[:, 128:256], in0=T.gy[:, 256:512:2], in1=T.gy[:, 257:512:2], op=A.add), [t_g1])
-    pre("p", [t_z1])
-    t_m1 = post("p", pe.matmul(T.pso1[:, 0:64], T.zz[:, 128:256], T.rsel[:], True, True))
-    pre("a", [t_m0])
-    post("a", sc.activation(T.ys[:, 0:64], T.pso0[:, 0:64], AF.Copy))
-    pre("a")
-    sc.dma_start(T.y[0:128, :], T.ys[:, 0:64]).then_inc(S.sy0, 16)
-    t_y1 = V(lambda: v.tensor_copy(T.ys[:, 64:128], T.pso1[:, 0:64]), [t_m1])
-    pre("y", [t_y1])
-    sy.dma_start(T.y[128:256, :], T.ys[:, 64:128]).then_inc(S.sy1, 16)
+    ready = [t_oy, t_own, t_lz, t_rsp]
+    f0 = one("v", lambda: v.tensor_copy(T.gy[:, 0:256], lwin.indirect(T.offy[:, 0:16])), ready)
+    f1 = one("a", lambda: sc.activation(T.gy[:, 256:512], lwin.indirect(T.offy[:, 16:32]), AF.Copy), ready)
+    z0 = one("v", lambda: v.tensor_tensor(out=T.zz[:, 0:128], in0=T.gy[:, 0:256:2], in1=T.gy[:, 1:256:2], op=A.add), [f0])
+    m0 = one("p", lambda: pe.matmul(T.pso0[:, 0:64], T.zz[:, 0:128], T.rsel[:], True, True), [z0, y3])
+    z1 = one("v", lambda: v.tensor_tensor(out=T.zz[:, 128:256], in0=T.gy[:, 256:512:2], in1=T.gy[:, 257:512:2], op=A.add), [f1])
+    m1 = one("p", lambda: pe.matmul(T.pso1[:, 0:64], T.zz[:, 128:256], T.rsel[:], True, True), [z1])
+    e0 = one("a", lambda: sc.activation(T.ys[:, 0:64], T.pso0[:, 0:64], AF.Copy), [m0])
+    emit("a", lambda: sc.dma_start(T.y[0:128, :], T.ys[:, 0:64]).then_inc(S.sy0, 16), [e0])
+    e1 = one("v", lambda: v.tensor_copy(T.ys[:, 64:128], T.pso1[:, 0:64]), [m1])
+    emit("y", lambda: sy.dma_start(T.y[128:256, :], T.ys[:, 64:128]).then_inc(S.sy1, 16), [e1])
 
-    fin = [(k, n) for k, n in cnt.items()] + [t_idx, t_rsp, ("lsem", lsem), ("sy0", 16), ("sy1", 16)]
-    fin += [("snat%d" % k, 16) for k in range(4)] + [("rq%d" % r, n) for r, n in nrq.items()]
-    pre("g", fin)
+    emit("g", lambda: g.wait_ge(S.lsem, lsem[0]), [("sy0", 16), ("sy1", 16)])

@@ -38,6 +38,7 @@ SEMAPHORES = (["sidx", "snat0", "snat1", "snat2", "snat3", "rsp", "lsem", "hq", 
               + ["rq%d" % r for r in range(16)] + ["x%d" % i for i in range(NSTAGE)])
 
 _CACHE = {}
+PASSED = ("far", "rack", "cable")
 
 
 def _bits(mask):
@@ -52,7 +53,7 @@ def _plan(T, topo):
     if "p" in _CACHE:
         return _CACHE["p"]
     cores = [int(x) for x in T.cores]
-    groups, relay, serves = {}, {}, {}
+    groups, passer, serves, eng = {}, {}, {}, {}
     for s in cores:
         gr = {"far": [], "cable": [], "rack": [], "same": []}
         for r, d in enumerate(cores):
@@ -67,15 +68,22 @@ def _plan(T, topo):
             else:
                 gr["cable"].append(r)
         groups[s] = gr
-        cand = [x for x in range(NCORES)
-                if T.rank_of(x) is None and topo.chip(x) == topo.chip(s)
-                and topo.rack(topo.host(x)) != topo.rack(topo.host(s)) and topo.may_write(s, x)
-                and all(topo.may_write(x, cores[r]) for r in gr["far"])]
-        cand.sort(key=lambda x: (topo.die(x) == topo.die(s), x))
-        relay[s] = cand[0:2]
-        for i, x in enumerate(relay[s]):
-            serves[x] = (s, i)
-    _CACHE["p"] = {"cores": cores, "groups": groups, "relay": relay, "serves": serves}
+        free = [x for x in range(NCORES) if T.rank_of(x) is None and topo.chip(x) == topo.chip(s) and topo.may_write(s, x)]
+        order = lambda x: (topo.die(x) != topo.die(s), x)
+        near = sorted([x for x in free if topo.host(x) == topo.host(s)
+                       and all(topo.may_write(x, cores[r]) for r in gr["rack"] + gr["cable"])], key=order)
+        away = sorted([x for x in free if topo.rack(topo.host(x)) != topo.rack(topo.host(s))
+                       and all(topo.may_write(x, cores[r]) for r in gr["far"])], key=order)
+        passer[s] = {"rack": near[0], "cable": near[1], "far": away[-1]}
+        off = _bits(topo.mask(s, away[-1]))
+        spare = [i for i in _bits(topo.mask(s, near[0])) if i not in off]
+        h = len(spare) // 2
+        eng[s] = {"far": (off, off), "rack": (spare[0:h], spare), "cable": (spare[h:2 * h], spare)}
+        for k in PASSED:
+            if passer[s][k] in serves:
+                raise ValueError("a passing core with two tasks")
+            serves[passer[s][k]] = (s, k)
+    _CACHE["p"] = {"cores": cores, "groups": groups, "passer": passer, "serves": serves, "eng": eng}
     return _CACHE["p"]
 
 
@@ -89,17 +97,15 @@ def _share(topo, a, b, n=4):
     return len(_bits(topo.mask(a, b))) // n
 
 
-def _relay(g, core, s, half, T, topo, plan):
+def _pass(g, core, s, kind, T, topo, plan):
     S, cores = T.sem, plan["cores"]
     sr = T.rank_of(s)
-    far = plan["groups"][s]["far"][2 * half:2 * half + 2]
-    nin = _share(topo, s, core, 2)
     tot = 0
-    for sem_in, sem_out, buf, land, w in ((S.hq, S["rq%d" % sr], T.reqx, T.offs, 4), (S.hr, S.rsp, T.gout, T.land, 64)):
-        g.wait_ge(sem_in, nin)
+    for ph, sem_in, sem_out, buf, land, w in ((0, S.hq, S["rq%d" % sr], T.reqx, T.offs, 4), (1, S.hr, S.rsp, T.gout, T.land, 64)):
+        g.wait_ge(sem_in, len(plan["eng"][s][kind][ph]))
         trs = []
-        for t, d in enumerate(far):
-            e = _share(topo, core, cores[d], 2)
+        for t, d in enumerate(plan["groups"][s][kind]):
+            e = _share(topo, core, cores[d])
             trs.append(_tr(topo, core, cores[d], t, e, sem_out, buf[:, w * d:w * d + w], land[:, w * sr:w * sr + w]))
             tot += e
         g.remote_dma_fused(trs, local_sem=S.hl)
@@ -112,12 +118,12 @@ def rank_program(g, core, T, topo):
     if me is None:
         s = plan["serves"].get(core)
         if s is not None:
-            _relay(g, core, s[0], s[1], T, topo, plan)
+            _pass(g, core, s[0], s[1], T, topo, plan)
         return
     S, cores = T.sem, plan["cores"]
     A, AF = AluOpType, ActivationFunctionType
     v, pe, sc, sy = g.vector, g.tensor, g.scalar, g.sync
-    grp, relay = plan["groups"][core], plan["relay"][core]
+    grp, passer = plan["groups"][core], plan["passer"][core]
     Q = {"v": v, "p": pe, "a": sc, "g": g, "y": sy}
     seen, nx = {}, [0]
 
@@ -219,15 +225,16 @@ def rank_program(g, core, T, topo):
     t_req = one("v", lambda: v.tensor_copy(T.reqx[:], T.psr[:, 0:64]), [s12])
 
     lsem = [0]
-    far = grp["far"]
 
-    def to_relays(buf, w, sem):
+    def hand(kinds, buf, w, sem, ph):
         trs = []
-        for i, x in enumerate(relay):
-            e = _share(topo, core, x, 2)
-            ap = buf[:, w * far[2 * i]:w * far[2 * i] + 2 * w]
-            trs.append(_tr(topo, core, x, i, e, sem, ap, ap))
-            lsem[0] += e
+        for kind in kinds:
+            rs, x, en = grp[kind], passer[kind], plan["eng"][core][kind][ph]
+            ap = buf[:, w * rs[0]:w * rs[0] + w * len(rs)]
+            rid, pid = topo.addr(x, core)
+            trs.append(RemoteDMATransfer(dst_ids=[DstId(rid=rid, pnc=pid)], dma_engine_mask=sum(1 << i for i in en),
+                                         remote_sem=sem, src=ap, dst=ap))
+            lsem[0] += len(en)
         return g.remote_dma_fused(trs, local_sem=S.lsem)
 
     def fan(rs, sem, buf, w, dst):
@@ -238,9 +245,9 @@ def rank_program(g, core, T, topo):
             lsem[0] += e
         return g.remote_dma_fused(trs, local_sem=S.lsem)
 
-    emit("g", lambda: to_relays(T.reqx, 4, S.hq), [t_req])
-    for kind in ("cable", "rack", "same"):
-        fan(grp[kind], S["rq%d" % me], T.reqx, 4, T.offs[:, 4 * me:4 * me + 4])
+    emit("g", lambda: hand(("far",), T.reqx, 4, S.hq, 0), [t_req])
+    hand(("rack", "cable"), T.reqx, 4, S.hq, 0)
+    fan(grp["same"], S["rq%d" % me], T.reqx, 4, T.offs[:, 4 * me:4 * me + 4])
 
     y1 = one("v", lambda: v.tensor_scalar(out=T.p15i[:], in0=T.pidx[:], scalar1=15, scalar2=None, op0=A.bitwise_and), [t_pi])
     y4 = stage()
@@ -273,23 +280,24 @@ def rank_program(g, core, T, topo):
     nrq = {}
     for r, d in enumerate(cores):
         if r != me:
-            isfar = me in plan["groups"][d]["far"]
-            nrq[r] = _share(topo, plan["relay"][d][0], core, 2) if isfar else _share(topo, d, core)
-    for kind in ("cable", "far", "rack", "same"):
+            last = d
+            for kind in PASSED:
+                if me in plan["groups"][d][kind]:
+                    last = plan["passer"][d][kind]
+            nrq[r] = _share(topo, last, core)
+    for kind in ("rack", "cable", "far", "same"):
         rs = grp[kind]
         deps = evb + [("rq%d" % r, nrq[r]) for r in rs]
         t_g = stage()
         if kind == "same":
             for r in rs:
                 emit("v", lambda: v.tensor_copy(T.gout[:, 64 * r:64 * r + 64], win.indirect(T.offs[:, 4 * r:4 * r + 4])), deps, t_g)
+            emit("g", lambda: fan(rs, S.rsp, T.gout, 64, T.land[:, 64 * me:64 * me + 64]), [t_g])
         else:
             r0 = rs[0]
             emit("v", lambda: v.tensor_copy(T.gout[:, 64 * r0:64 * r0 + 256], win.indirect(T.offs[:, 4 * r0:4 * r0 + 16])),
                  deps, t_g)
-        if kind == "far":
-            emit("g", lambda: to_relays(T.gout, 64, S.hr), [t_g])
-        else:
-            emit("g", lambda: fan(rs, S.rsp, T.gout, 64, T.land[:, 64 * me:64 * me + 64]), [t_g])
+            emit("g", lambda: hand((kind,), T.gout, 64, S.hr, 1), [t_g])
     t_own = one("v", lambda: v.tensor_copy(T.land[:, 64 * me:64 * me + 64], win.indirect(T.reqx[:, 4 * me:4 * me + 4])), [t_req])
     t_oy = one("v", lambda: v.tensor_scalar(out=T.offy[:], in0=T.psr[:, 64:96], scalar1=1024.0, scalar2=None, op0=A.add), [y8])
 

@@ -2,7 +2,7 @@ from concourse.bass import DstId, RemoteDMATransfer
 from concourse.mybir import AluOpType, ActivationFunctionType
 
 NCORES = 512
-NPRE = 1
+NPRE = 3
 NSTAGE = 64
 
 
@@ -38,7 +38,7 @@ SEMAPHORES = (["sidx", "snat0", "snat1", "snat2", "snat3", "rsp", "lsem", "hq", 
               + ["rq%d" % r for r in range(16)] + ["x%d" % i for i in range(NSTAGE)])
 
 _CACHE = {}
-PASSED = ("far", "rack", "cable")
+PASSED = ("far0", "far1", "rack", "cable")
 
 
 def _bits(mask):
@@ -54,6 +54,7 @@ def _plan(T, topo):
         return _CACHE["p"]
     cores = [int(x) for x in T.cores]
     groups, passer, serves, eng = {}, {}, {}, {}
+    taken = set((topo.host(d), topo.chip(d)) for d in cores)
     for s in cores:
         gr = {"far": [], "cable": [], "rack": [], "same": []}
         for r, d in enumerate(cores):
@@ -67,6 +68,7 @@ def _plan(T, topo):
                 gr["rack"].append(r)
             else:
                 gr["cable"].append(r)
+        gr["far0"], gr["far1"] = gr["far"][0:2], gr["far"][2:4]
         groups[s] = gr
         free = [x for x in range(NCORES) if T.rank_of(x) is None and topo.chip(x) == topo.chip(s) and topo.may_write(s, x)]
         order = lambda x: (topo.die(x) != topo.die(s), x)
@@ -74,11 +76,17 @@ def _plan(T, topo):
                        and all(topo.may_write(x, cores[r]) for r in gr["rack"] + gr["cable"])], key=order)
         away = sorted([x for x in free if topo.rack(topo.host(x)) != topo.rack(topo.host(s))
                        and all(topo.may_write(x, cores[r]) for r in gr["far"])], key=order)
-        passer[s] = {"rack": near[0], "cable": near[1], "far": away[-1]}
+        plane = sorted([x for x in range(NCORES) if T.rank_of(x) is None and topo.same_plane(s, x) and topo.may_write(s, x)
+                        and topo.host(x) != topo.host(s) and (topo.host(x), topo.chip(x)) not in taken
+                        and all(topo.may_write(x, cores[r]) for r in gr["far1"])], key=order)
+        taken.add((topo.host(plane[0]), topo.chip(plane[0])))
+        passer[s] = {"rack": near[0], "cable": near[1], "far0": away[-1], "far1": plane[0]}
         off = _bits(topo.mask(s, away[-1]))
+        q = len(off) // 2
         spare = [i for i in _bits(topo.mask(s, near[0])) if i not in off]
         h = len(spare) // 2
-        eng[s] = {"far": (off, off), "rack": (spare[0:h], spare), "cable": (spare[h:2 * h], spare)}
+        eng[s] = {"far0": (off[0:q], off[0:q]), "far1": (off[q:2 * q], off[q:2 * q]),
+                  "rack": (spare[0:h], spare), "cable": (spare[h:2 * h], spare)}
         for k in PASSED:
             if passer[s][k] in serves:
                 raise ValueError("a passing core with two tasks")
@@ -94,7 +102,14 @@ def _tr(topo, src_core, dst_core, t, e, sem, src, dst):
 
 
 def _share(topo, a, b, n=4):
-    return len(_bits(topo.mask(a, b))) // n
+    p = 1
+    while p < n:
+        p *= 2
+    return len(_bits(topo.mask(a, b))) // p
+
+
+def _waves(rs):
+    return [rs[0:2], rs[2:3]] if len(rs) == 3 else [rs]
 
 
 def _pass(g, core, s, kind, T, topo, plan):
@@ -104,8 +119,9 @@ def _pass(g, core, s, kind, T, topo, plan):
     for ph, sem_in, sem_out, buf, land, w in ((0, S.hq, S["rq%d" % sr], T.reqx, T.offs, 4), (1, S.hr, S.rsp, T.gout, T.land, 64)):
         g.wait_ge(sem_in, len(plan["eng"][s][kind][ph]))
         trs = []
-        for t, d in enumerate(plan["groups"][s][kind]):
-            e = _share(topo, core, cores[d])
+        ds = plan["groups"][s][kind]
+        for t, d in enumerate(ds):
+            e = _share(topo, core, cores[d], len(ds))
             trs.append(_tr(topo, core, cores[d], t, e, sem_out, buf[:, w * d:w * d + w], land[:, w * sr:w * sr + w]))
             tot += e
         g.remote_dma_fused(trs, local_sem=S.hl)
@@ -238,14 +254,15 @@ def rank_program(g, core, T, topo):
         return g.remote_dma_fused(trs, local_sem=S.lsem)
 
     def fan(rs, sem, buf, w, dst):
-        trs = []
-        for t, d in enumerate(rs):
-            e = _share(topo, core, cores[d])
-            trs.append(_tr(topo, core, cores[d], t, e, sem, buf[:, w * d:w * d + w], dst))
-            lsem[0] += e
-        return g.remote_dma_fused(trs, local_sem=S.lsem)
+        for wave in _waves(rs):
+            trs = []
+            for t, d in enumerate(wave):
+                e = _share(topo, core, cores[d], len(wave))
+                trs.append(_tr(topo, core, cores[d], t, e, sem, buf[:, w * d:w * d + w], dst))
+                lsem[0] += e
+            g.remote_dma_fused(trs, local_sem=S.lsem)
 
-    emit("g", lambda: hand(("far",), T.reqx, 4, S.hq, 0), [t_req])
+    emit("g", lambda: hand(("far0", "far1"), T.reqx, 4, S.hq, 0), [t_req])
     hand(("rack", "cable"), T.reqx, 4, S.hq, 0)
     fan(grp["same"], S["rq%d" % me], T.reqx, 4, T.offs[:, 4 * me:4 * me + 4])
 
@@ -280,11 +297,14 @@ def rank_program(g, core, T, topo):
     nrq = {}
     for r, d in enumerate(cores):
         if r != me:
-            last = d
+            last, n = d, 0
+            for wave in _waves(plan["groups"][d]["same"]):
+                if me in wave:
+                    n = len(wave)
             for kind in PASSED:
                 if me in plan["groups"][d][kind]:
-                    last = plan["passer"][d][kind]
-            nrq[r] = _share(topo, last, core)
+                    last, n = plan["passer"][d][kind], len(plan["groups"][d][kind])
+            nrq[r] = _share(topo, last, core, n)
     for kind in ("rack", "cable", "far", "same"):
         rs = grp[kind]
         deps = evb + [("rq%d" % r, nrq[r]) for r in rs]
@@ -297,7 +317,7 @@ def rank_program(g, core, T, topo):
             r0 = rs[0]
             emit("v", lambda: v.tensor_copy(T.gout[:, 64 * r0:64 * r0 + 256], win.indirect(T.offs[:, 4 * r0:4 * r0 + 16])),
                  deps, t_g)
-            emit("g", lambda: hand((kind,), T.gout, 64, S.hr, 1), [t_g])
+            emit("g", lambda: hand(("far0", "far1") if kind == "far" else (kind,), T.gout, 64, S.hr, 1), [t_g])
     t_own = one("v", lambda: v.tensor_copy(T.land[:, 64 * me:64 * me + 64], win.indirect(T.reqx[:, 4 * me:4 * me + 4])), [t_req])
     t_oy = one("v", lambda: v.tensor_scalar(out=T.offy[:], in0=T.psr[:, 64:96], scalar1=1024.0, scalar2=None, op0=A.add), [y8])
 

@@ -2,7 +2,7 @@ from concourse.bass import DstId, RemoteDMATransfer
 from concourse.mybir import AluOpType, ActivationFunctionType
 
 NCORES = 512
-NPRE = 3
+NPRE = 4
 NSTAGE = 64
 
 
@@ -38,7 +38,7 @@ SEMAPHORES = (["sidx", "snat0", "snat1", "snat2", "snat3", "rsp", "lsem", "hq", 
               + ["rq%d" % r for r in range(16)] + ["x%d" % i for i in range(NSTAGE)])
 
 _CACHE = {}
-PASSED = ("far0", "far1", "rack", "cable")
+PASSED = ("far0", "far1", "rack0", "rack1", "cable0", "cable1")
 
 
 def _bits(mask):
@@ -46,14 +46,15 @@ def _bits(mask):
 
 
 def _sub(mask, t, e):
-    return sum(1 << i for i in _bits(mask)[t * e:(t + 1) * e])
+    b = _bits(mask)
+    return sum(1 << i for i in b[t::len(b) // e])
 
 
 def _plan(T, topo):
     if "p" in _CACHE:
         return _CACHE["p"]
     cores = [int(x) for x in T.cores]
-    groups, passer, serves, eng = {}, {}, {}, {}
+    groups, passer, serves, eng, pos = {}, {}, {}, {}, {}
     taken = set((topo.host(d), topo.chip(d)) for d in cores)
     for s in cores:
         gr = {"far": [], "cable": [], "rack": [], "same": []}
@@ -80,18 +81,28 @@ def _plan(T, topo):
                         and topo.host(x) != topo.host(s) and (topo.host(x), topo.chip(x)) not in taken
                         and all(topo.may_write(x, cores[r]) for r in gr["far1"])], key=order)
         taken.add((topo.host(plane[0]), topo.chip(plane[0])))
-        passer[s] = {"rack": near[0], "cable": near[1], "far0": away[-1], "far1": plane[0]}
+        plain = sorted([x for x in free if topo.host(x) == topo.host(s) and x not in near], key=order)
+        passer[s] = {"rack0": plain[-2], "rack1": near[0], "cable0": plain[-1], "cable1": near[1],
+                     "far0": away[-1], "far1": plane[0]}
+        pos[s] = dict((r, r) for r in range(len(cores)))
+        for k in ("rack", "cable"):
+            gr[k + "0"] = [r for r in gr[k] if topo.may_write(passer[s][k + "0"], cores[r])]
+            gr[k + "1"] = [r for r in gr[k] if r not in gr[k + "0"]]
+            if len(gr[k + "0"]) != len(gr[k + "1"]):
+                raise ValueError("uneven halves")
+            for i, r in enumerate(gr[k + "0"] + gr[k + "1"]):
+                pos[s][r] = gr[k][0] + i
         off = _bits(topo.mask(s, away[-1]))
-        q = len(off) // 2
         spare = [i for i in _bits(topo.mask(s, near[0])) if i not in off]
-        h = len(spare) // 2
-        eng[s] = {"far0": (off[0:q], off[0:q]), "far1": (off[q:2 * q], off[q:2 * q]),
-                  "rack": (spare[0:h], spare), "cable": (spare[h:2 * h], spare)}
+        e = len(spare) // 4
+        eng[s] = {"far0": (off[0::2], off[0::2]), "far1": (off[1::2], off[1::2]),
+                  "rack0": (spare[0:e], spare[0::2]), "rack1": (spare[e:2 * e], spare[1::2]),
+                  "cable0": (spare[2 * e:3 * e], spare[0::2]), "cable1": (spare[3 * e:4 * e], spare[1::2])}
         for k in PASSED:
             if passer[s][k] in serves:
                 raise ValueError("a passing core with two tasks")
             serves[passer[s][k]] = (s, k)
-    _CACHE["p"] = {"cores": cores, "groups": groups, "passer": passer, "serves": serves, "eng": eng}
+    _CACHE["p"] = {"cores": cores, "groups": groups, "passer": passer, "serves": serves, "eng": eng, "pos": pos}
     return _CACHE["p"]
 
 
@@ -122,7 +133,9 @@ def _pass(g, core, s, kind, T, topo, plan):
         ds = plan["groups"][s][kind]
         for t, d in enumerate(ds):
             e = _share(topo, core, cores[d], len(ds))
-            trs.append(_tr(topo, core, cores[d], t, e, sem_out, buf[:, w * d:w * d + w], land[:, w * sr:w * sr + w]))
+            a = d if ph == 0 else plan["pos"][s][d]
+            b = plan["pos"][cores[d]][sr] if ph == 0 else sr
+            trs.append(_tr(topo, core, cores[d], t, e, sem_out, buf[:, w * a:w * a + w], land[:, w * b:w * b + w]))
             tot += e
         g.remote_dma_fused(trs, local_sem=S.hl)
     g.wait_ge(S.hl, tot)
@@ -163,7 +176,7 @@ def rank_program(g, core, T, topo):
 
     sy.dma_start(T.idxs[:], T.idx[:]).then_inc(S.sidx, 16)
     for k in range(4):
-        (sy if k % 2 == 0 else sc).dma_start(T["nat%d" % k][:], T.tab[1024 * k:1024 * (k + 1), :]).then_inc(S["snat%d" % k], 16)
+        (sc if k % 2 == 0 else sy).dma_start(T["nat%d" % k][:], T.tab[1024 * k:1024 * (k + 1), :]).then_inc(S["snat%d" % k], 16)
     t_idx = ("sidx", 16)
 
     t_ob = one("v", lambda: v.memset(T.onesb[:], 1.0))
@@ -245,8 +258,12 @@ def rank_program(g, core, T, topo):
     def hand(kinds, buf, w, sem, ph):
         trs = []
         for kind in kinds:
-            rs, x, en = grp[kind], passer[kind], plan["eng"][core][kind][ph]
-            ap = buf[:, w * rs[0]:w * rs[0] + w * len(rs)]
+            x, en = passer[kind], plan["eng"][core][kind][ph]
+            if ph == 0:
+                ps = grp[kind] if kind in ("far0", "far1") else grp[kind[:-1]]
+            else:
+                ps = sorted(plan["pos"][core][r] for r in grp[kind])
+            ap = buf[:, w * ps[0]:w * ps[0] + w * len(ps)]
             rid, pid = topo.addr(x, core)
             trs.append(RemoteDMATransfer(dst_ids=[DstId(rid=rid, pnc=pid)], dma_engine_mask=sum(1 << i for i in en),
                                          remote_sem=sem, src=ap, dst=ap))
@@ -263,7 +280,7 @@ def rank_program(g, core, T, topo):
             g.remote_dma_fused(trs, local_sem=S.lsem)
 
     emit("g", lambda: hand(("far0", "far1"), T.reqx, 4, S.hq, 0), [t_req])
-    hand(("rack", "cable"), T.reqx, 4, S.hq, 0)
+    hand(("rack0", "rack1", "cable0", "cable1"), T.reqx, 4, S.hq, 0)
     fan(grp["same"], S["rq%d" % me], T.reqx, 4, T.offs[:, 4 * me:4 * me + 4])
 
     y1 = one("v", lambda: v.tensor_scalar(out=T.p15i[:], in0=T.pidx[:], scalar1=15, scalar2=None, op0=A.bitwise_and), [t_pi])
@@ -305,19 +322,23 @@ def rank_program(g, core, T, topo):
                 if me in plan["groups"][d][kind]:
                     last, n = plan["passer"][d][kind], len(plan["groups"][d][kind])
             nrq[r] = _share(topo, last, core, n)
-    for kind in ("rack", "cable", "far", "same"):
+    for kind in ("rack", "far", "cable", "same"):
         rs = grp[kind]
         deps = evb + [("rq%d" % r, nrq[r]) for r in rs]
         t_g = stage()
         if kind == "same":
             for r in rs:
-                emit("v", lambda: v.tensor_copy(T.gout[:, 64 * r:64 * r + 64], win.indirect(T.offs[:, 4 * r:4 * r + 4])), deps, t_g)
+                emit("a", lambda: sc.activation(T.gout[:, 64 * r:64 * r + 64], win.indirect(T.offs[:, 4 * r:4 * r + 4]), AF.Copy),
+                     deps, t_g)
             emit("g", lambda: fan(rs, S.rsp, T.gout, 64, T.land[:, 64 * me:64 * me + 64]), [t_g])
         else:
             r0 = rs[0]
-            emit("v", lambda: v.tensor_copy(T.gout[:, 64 * r0:64 * r0 + 256], win.indirect(T.offs[:, 4 * r0:4 * r0 + 16])),
-                 deps, t_g)
-            emit("g", lambda: hand(("far0", "far1") if kind == "far" else (kind,), T.gout, 64, S.hr, 1), [t_g])
+            out, src = T.gout[:, 64 * r0:64 * r0 + 256], win.indirect(T.offs[:, 4 * r0:4 * r0 + 16])
+            if kind == "far":
+                emit("a", lambda: sc.activation(out, src, AF.Copy), deps, t_g)
+            else:
+                emit("v", lambda: v.tensor_copy(out, src), deps, t_g)
+            emit("g", lambda: hand((kind + "0", kind + "1"), T.gout, 64, S.hr, 1), [t_g])
     t_own = one("v", lambda: v.tensor_copy(T.land[:, 64 * me:64 * me + 64], win.indirect(T.reqx[:, 4 * me:4 * me + 4])), [t_req])
     t_oy = one("v", lambda: v.tensor_scalar(out=T.offy[:], in0=T.psr[:, 64:96], scalar1=1024.0, scalar2=None, op0=A.add), [y8])
 

@@ -2,8 +2,8 @@ from concourse.bass import DstId, RemoteDMATransfer
 from concourse.mybir import AluOpType, ActivationFunctionType
 
 NCORES = 512
-NPRE = 4
-NSTAGE = 64
+NPRE = 2
+NSTAGE = 72
 
 
 def _sb(shape, dtype="float32"):
@@ -12,21 +12,24 @@ def _sb(shape, dtype="float32"):
 
 SCRATCH = {
     "idxs": _sb([128, 4], "int32"),
-    "nat0": _sb([128, 512]), "nat1": _sb([128, 512]), "nat2": _sb([128, 512]), "nat3": _sb([128, 512]),
+    "nat0": _sb([128, 256]), "nat1": _sb([128, 256]), "nat2": _sb([128, 512]), "nat3": _sb([128, 512]),
+    "nat4": _sb([128, 256]), "nat5": _sb([128, 256]),
     "tabT": _sb([128, 4096]),
-    "ident": _sb([128, 128]), "onesf": _sb([128, 128]), "io128": _sb([128, 128]), "kcode": _sb([128, 128]),
-    "onesb": _sb([128, 128], "bfloat16"), "lstr": _sb([128, 128], "bfloat16"), "cstb": _sb([128, 64], "bfloat16"),
+    "ident": _sb([128, 128]), "onesf": _sb([128, 128]),
+    "kc2": _sb([128, 128], "bfloat16"), "nc64": _sb([128, 64], "bfloat16"), "thr64": _sb([128, 64], "bfloat16"),
+    "twosb": _sb([128, 128], "bfloat16"), "lstr": _sb([128, 128], "bfloat16"), "lstr2": _sb([128, 128], "bfloat16"),
+    "cstb": _sb([128, 64], "bfloat16"), "biasb": _sb([128, 64], "bfloat16"),
     "segm": _sb([128, 64]), "e8a": _sb([128, 8]), "e8": _sb([128, 8]), "rsel": _sb([128, 64]),
     "pidx": _sb([128, 1], "int32"), "p15i": _sb([128, 1], "int32"), "p15f": _sb([128, 1]),
-    "oi8": _sb([128, 8], "int32"), "of8": _sb([128, 8]),
+    "ob": _sb([128, 4], "bfloat16"), "ri": _sb([128, 4], "int32"), "rowm": _sb([128, 4]),
     "hb": _sb([128, 64], "bfloat16"), "hcum": _sb([128, 192], "bfloat16"),
-    "prod": _sb([128, 64]), "seg": _sb([128, 64]),
-    "sloti": _sb([128, 4], "int32"), "kni": _sb([128, 8], "int32"), "knf": _sb([128, 8]),
-    "amat": _sb([128, 512]), "bmat": _sb([128, 256]),
+    "segf": _sb([128, 64]), "segb": _sb([128, 64], "bfloat16"), "nf": _sb([128, 4]),
+    "sloti": _sb([128, 4], "int32"),
+    "amat": _sb([128, 512], "float16"), "bmat": _sb([128, 256], "float16"),
     "reqx": _sb([128, 64], "uint16"), "offs": _sb([128, 64], "uint16"),
     "t16": _sb([128, 4], "int32"), "u15": _sb([128, 4], "int32"), "u15f": _sb([128, 4]),
     "keyy": _sb([128, 4]), "valn": _sb([128, 4]), "valy": _sb([128, 4]),
-    "aymat": _sb([128, 512]), "bymat": _sb([128, 32]), "offy": _sb([128, 32], "uint16"),
+    "aymat": _sb([128, 512], "float16"), "bymat": _sb([128, 32], "float16"), "offy": _sb([128, 32], "uint16"),
     "gout": _sb([128, 1024]), "land": _sb([128, 1028]),
     "gy": _sb([128, 512]), "zz": _sb([128, 256]), "ys": _sb([128, 128]),
     "pst0": ("psum", [128, 512], "float32"), "pst1": ("psum", [128, 512], "float32"),
@@ -34,7 +37,7 @@ SCRATCH = {
     "psp": ("psum", [128, 512], "float32"), "psr": ("psum", [128, 512], "float32"),
     "pso0": ("psum", [128, 512], "float32"), "pso1": ("psum", [128, 512], "float32"),
 }
-SEMAPHORES = (["sidx", "snat0", "snat1", "snat2", "snat3", "rsp", "lsem", "hq", "hr", "hl", "sy0", "sy1"]
+SEMAPHORES = (["sidx", "snat0", "snat1", "snat2", "snat3", "snat4", "snat5", "rsp", "lsem", "hq", "hr", "hl", "sy0", "sy1"]
               + ["rq%d" % r for r in range(16)] + ["x%d" % i for i in range(NSTAGE)])
 
 _CACHE = {}
@@ -174,22 +177,27 @@ def rank_program(g, core, T, topo):
     def one(qn, fn, deps=()):
         return emit(qn, fn, deps, stage())
 
+    pieces = [(0, 512), (512, 512), (1024, 1024), (2048, 1024), (3072, 512), (3584, 512)]
     sy.dma_start(T.idxs[:], T.idx[:]).then_inc(S.sidx, 16)
-    for k in range(4):
-        (sc if k % 2 == 0 else sy).dma_start(T["nat%d" % k][:], T.tab[1024 * k:1024 * (k + 1), :]).then_inc(S["snat%d" % k], 16)
+    for k, (r0, nr) in enumerate(pieces):
+        (sc if k % 2 == 0 else sy).dma_start(T["nat%d" % k][:], T.tab[r0:r0 + nr, :]).then_inc(S["snat%d" % k], 16)
     t_idx = ("sidx", 16)
+    blocks = [(k, u) for k, (r0, nr) in enumerate(pieces) for u in range(nr // 256)]
 
-    t_ob = one("v", lambda: v.memset(T.onesb[:], 1.0))
+    t_tw = one("v", lambda: v.memset(T.twosb[:], 2.0))
     t_of = one("v", lambda: v.memset(T.onesf[:], 1.0))
+    t_bi = one("v", lambda: v.memset(T.biasb[:], -31.0 / 256.0))
     t_hz = stage()
     for a, b in ((0, 16), (64, 96), (128, 176)):
         emit("v", lambda: v.memset(T.hcum[:, a:b], 0.0), (), t_hz)
     t_lz = one("v", lambda: v.memset(T.land[:, 1024:1028], 0.0))
-    t_io = one("g", lambda: g.iota(T.io128[:], [[1, 128]], 0, 0, allow_small_or_imprecise_dtypes=True))
+    t_th = one("g", lambda: g.iota(T.thr64[:], [[0, 4], [4096, 16]], 786432, 0, allow_small_or_imprecise_dtypes=True))
     t_cst = one("g", lambda: g.iota(T.cstb[:], [[0, 4], [1, 16]], 0, 0, allow_small_or_imprecise_dtypes=True))
-    t_l = one("g", lambda: g.affine_select(T.lstr[:], T.onesb[:], [[1, 128]], A.is_ge, 0.0, -1, -1), [t_ob])
+    t_l = one("g", lambda: g.affine_select(T.lstr[:], T.twosb[:], [[1, 128]], A.is_ge, 0.0, -1, -1), [t_tw])
+    t_l2 = one("g", lambda: g.affine_select(T.lstr2[:], T.lstr[:], [[1, 128]], A.not_equal, 9216.0, 0, -1), [t_l])
     t_id = one("g", lambda: g.affine_select(T.ident[:], T.onesf[:], [[-1, 128]], A.is_equal, 0.0, 0, 1), [t_of])
-    t_kc = one("g", lambda: g.iota(T.kcode[:], [[16, 2], [0, 4], [1, 16]], 0, 0, allow_small_or_imprecise_dtypes=True))
+    t_kc = one("g", lambda: g.iota(T.kc2[:], [[32, 2], [0, 4], [2, 16]], -31, 0, allow_small_or_imprecise_dtypes=True))
+    t_nc = one("g", lambda: g.iota(T.nc64[:], [[64, 64]], 9216, 0, allow_small_or_imprecise_dtypes=True))
     t_e8a = one("g", lambda: g.affine_select(T.e8a[:], T.onesf[:, 0:8], [[-16, 8]], A.is_ge, 0.0, 0, 1))
     t_e8 = one("g", lambda: g.affine_select(T.e8[:], T.e8a[:], [[16, 8]], A.is_ge, 0.0, 15, -1), [t_e8a])
     t_pi = one("g", lambda: g.iota(T.pidx[:], [[0, 1]], 0, 1))
@@ -199,59 +207,55 @@ def rank_program(g, core, T, topo):
     evb = [stage() for b in range(4)]
 
     def do_T(n):
-        k, u = divmod(n, 4)
+        k, u = blocks[n]
         emit("p", lambda: pe.transpose(T["pst%d" % (n % 4)][:, 0:128], T["nat%d" % k][:, 128 * u:128 * u + 128], T.ident[:]),
              [("snat%d" % k, 16), t_id, evb[n % 4]], tb[n % 4])
 
     def do_E(n):
-        k, u = divmod(n, 4)
-        qn = "v" if (n >= 8 and n % 2 == 0) else "a"
+        k, u = blocks[n]
+        r0, nr = pieces[k]
+        qn = "v" if (n >= NPRE and n % 2 == 1) else "a"
         for h in (0, 1):
             for dup in (0, 1):
-                out = T.tabT[64 * dup:64 * dup + 64, 1024 * k + 2 * u + h:1024 * (k + 1):8]
+                out = T.tabT[64 * dup:64 * dup + 64, r0 + 2 * u + h:r0 + nr:nr // 128]
                 in_ = T["pst%d" % (n % 4)][64 * h:64 * h + 64, 0:128]
                 emit(qn, lambda: v.tensor_copy(out, in_) if qn == "v" else sc.activation(out, in_, AF.Copy),
                      [tb[n % 4]], evb[n % 4])
 
-    s1 = stage()
-    emit("v", lambda: v.tensor_scalar(out=T.oi8[:, 0:4], in0=T.idxs[:], scalar1=12, scalar2=None, op0=A.logical_shift_right),
-         [t_idx], s1)
-    emit("v", lambda: v.tensor_scalar(out=T.oi8[:, 4:8], in0=T.idxs[:], scalar1=4095, scalar2=None, op0=A.bitwise_and), (), s1)
-    s2 = one("v", lambda: v.tensor_copy(T.of8[:], T.oi8[:]), [s1])
+    s1 = one("v", lambda: v.tensor_scalar(out=T.ob[:], in0=T.idxs[:], scalar1=784384.5, scalar2=None, op0=A.add), [t_idx])
+    r1 = one("v", lambda: v.tensor_scalar(out=T.ri[:], in0=T.idxs[:], scalar1=4095, scalar2=None, op0=A.bitwise_and))
     s3, s4 = stage(), stage()
     for c in range(4):
-        emit("v", lambda: v.tensor_scalar(out=T.hb[:, 16 * c:16 * c + 16], in0=T.io128[:, 0:16], scalar1=T.of8[:, c:c + 1],
-                                          scalar2=None, op0=A.is_equal), [s2, t_io], s3)
+        emit("v", lambda: v.tensor_scalar(out=T.hb[:, 16 * c:16 * c + 16], in0=T.thr64[:, 0:16], scalar1=T.ob[:, c:c + 1],
+                                          scalar2=None, op0=A.is_equal), [s1, t_th], s3)
     for c in range(3):
-        emit("v", lambda: v.tensor_scalar(out=T.hcum[:, 64 * c + 16 * (c + 1):64 * c + 64], in0=T.cstb[:, 0:48 - 16 * c],
-                                          scalar1=T.of8[:, c:c + 1], scalar2=None, op0=A.is_equal), [t_cst], s4)
-    emit("p", lambda: pe.matmul(T.psp[:, 0:64], T.onesb[:], T.cstb[:], True, False), [t_ob, t_cst])
-    emit("p", lambda: pe.matmul(T.psp[:, 0:64], T.lstr[:], T.hb[:], False, False), [t_l, s3])
+        emit("v", lambda: v.tensor_scalar(out=T.hcum[:, 64 * c + 16 * (c + 1):64 * c + 64], in0=T.thr64[:, 0:48 - 16 * c],
+                                          scalar1=T.ob[:, c:c + 1], scalar2=None, op0=A.is_equal), (), s4)
+    r2 = one("v", lambda: v.tensor_scalar(out=T.rowm[:], in0=T.ri[:], scalar1=-2048.0, scalar2=None, op0=A.add), [r1])
+    emit("p", lambda: pe.matmul(T.psp[:, 0:64], T.twosb[:], T.cstb[:], True, False), [t_tw, t_cst])
+    emit("p", lambda: pe.matmul(T.psp[:, 0:64], T.twosb[:], T.biasb[:], False, False), [t_bi])
+    emit("p", lambda: pe.matmul(T.psp[:, 0:64], T.lstr2[:], T.hb[:], False, False), [t_l2, s3])
     s5 = stage()
     for c in range(3):
-        emit("p", lambda: pe.matmul(T.psp[:, 0:64], T.onesb[:], T.hcum[:, 64 * c:64 * c + 64], False, c == 2), [s4, t_hz],
+        emit("p", lambda: pe.matmul(T.psp[:, 0:64], T.twosb[:], T.hcum[:, 64 * c:64 * c + 64], False, c == 2), [s4, t_hz],
              s5 if c == 2 else None)
     for n in range(NPRE):
         do_T(n)
         do_E(n)
-    s6 = one("v", lambda: v.tensor_tensor(out=T.prod[:], in0=T.psp[:, 0:64], in1=T.hb[:], op=A.mult), [s5, s3])
-    s7 = one("v", lambda: v.tensor_tensor_scan(T.seg[:], T.segm[:], T.prod[:], 0.0, A.mult, A.add), [s6, t_sg])
-    s8 = one("v", lambda: v.tensor_copy(T.sloti[:], T.seg[:, 15:64:16]), [s7])
-    s9 = stage()
-    emit("v", lambda: v.tensor_scalar(out=T.kni[:, 0:4], in0=T.sloti[:], scalar1=31, scalar2=None, op0=A.bitwise_and), [s8], s9)
-    emit("v", lambda: v.tensor_scalar(out=T.kni[:, 4:8], in0=T.sloti[:], scalar1=5, scalar2=None, op0=A.logical_shift_right),
-         (), s9)
-    s10 = one("v", lambda: v.tensor_copy(T.knf[:], T.kni[:]), [s9])
+    s6 = one("v", lambda: v.tensor_tensor_scan(T.segb[:], T.segm[:], T.psp[:, 0:64], 0.0, A.mult, A.max), [s5, t_sg])
+    s7 = one("v", lambda: v.tensor_tensor_scan(T.segf[:], T.segm[:], T.psp[:, 0:64], 0.0, A.mult, A.max))
+    s8 = one("v", lambda: v.tensor_copy(T.nf[:], T.segb[:, 15:64:16]), [s6])
     s12 = stage()
     for c in range(4):
         s11 = stage()
-        emit("v", lambda: v.tensor_scalar(out=T.amat[:, 128 * c:128 * c + 128], in0=T.kcode[:], scalar1=T.knf[:, c:c + 1],
-                                          scalar2=None, op0=A.is_equal), [s10, t_kc], s11)
-        emit("v", lambda: v.tensor_scalar(out=T.bmat[:, 64 * c:64 * c + 64], in0=T.io128[:, 0:64], scalar1=T.knf[:, 4 + c:5 + c],
-                                          scalar2=T.of8[:, 4 + c:5 + c], op0=A.is_equal, op1=A.mult), (), s11)
+        e = 16 * c + 15
+        emit("v", lambda: v.tensor_scalar(out=T.amat[:, 128 * c:128 * c + 128], in0=T.kc2[:], scalar1=T.nf[:, c:c + 1],
+                                          scalar2=T.segf[:, e:e + 1], op0=A.add, op1=A.is_equal), [s7, s8, t_kc], s11)
+        emit("v", lambda: v.tensor_scalar(out=T.bmat[:, 64 * c:64 * c + 64], in0=T.nc64[:], scalar1=T.nf[:, c:c + 1],
+                                          scalar2=T.rowm[:, c:c + 1], op0=A.is_equal, op1=A.mult), [t_nc, r2], s11)
         emit("p", lambda: pe.matmul(T.psr[:, 0:64], T.amat[:, 128 * c:128 * c + 128], T.bmat[:, 64 * c:64 * c + 64],
                                     c == 0, c == 3), [s11], s12 if c == 3 else None)
-    t_req = one("v", lambda: v.tensor_copy(T.reqx[:], T.psr[:, 0:64]), [s12])
+    t_req = one("v", lambda: v.tensor_scalar(out=T.reqx[:], in0=T.psr[:, 0:64], scalar1=2048.0, scalar2=None, op0=A.add), [s12])
 
     lsem = [0]
 
@@ -283,32 +287,9 @@ def rank_program(g, core, T, topo):
     hand(("rack0", "rack1", "cable0", "cable1"), T.reqx, 4, S.hq, 0)
     fan(grp["same"], S["rq%d" % me], T.reqx, 4, T.offs[:, 4 * me:4 * me + 4])
 
-    y1 = one("v", lambda: v.tensor_scalar(out=T.p15i[:], in0=T.pidx[:], scalar1=15, scalar2=None, op0=A.bitwise_and), [t_pi])
-    y4 = stage()
-    emit("v", lambda: v.tensor_scalar(out=T.t16[:], in0=T.sloti[:], scalar1=16, scalar2=None, op0=A.bitwise_and), (), y4)
-    emit("v", lambda: v.tensor_scalar(out=T.u15[:], in0=T.sloti[:], scalar1=15, scalar2=None, op0=A.bitwise_and), (), y4)
-    y3 = one("v", lambda: v.tensor_tensor(out=T.rsel[:], in0=T.ident[:, 0:64], in1=T.ident[:, 64:128], op=A.add), [t_id])
-    y2 = one("v", lambda: v.tensor_copy(T.p15f[:], T.p15i[:]), [y1])
-    y5 = stage()
-    emit("v", lambda: v.tensor_scalar(out=T.keyy[:], in0=T.t16[:], scalar1=T.p15f[:, 0:1], scalar2=None, op0=A.add), [y4, y2], y5)
-    emit("v", lambda: v.tensor_copy(T.u15f[:], T.u15[:]), (), y5)
-    emit("v", lambda: v.tensor_scalar(out=T.valn[:], in0=T.knf[:, 4:8], scalar1=16.0, scalar2=-1024.0, op0=A.mult, op1=A.add),
-         (), y5)
-    y6 = one("v", lambda: v.tensor_tensor(out=T.valy[:], in0=T.valn[:], in1=T.u15f[:], op=A.add), [y5])
-    y7 = stage()
-    for c in range(4):
-        emit("v", lambda: v.tensor_scalar(out=T.aymat[:, 128 * c:128 * c + 128], in0=T.kcode[:], scalar1=T.keyy[:, c:c + 1],
-                                          scalar2=None, op0=A.is_equal), (), y7)
-        emit("v", lambda: v.tensor_scalar(out=T.bymat[:, 8 * c:8 * c + 8], in0=T.e8[:], scalar1=T.valy[:, c:c + 1],
-                                          scalar2=None, op0=A.mult), [y6, t_e8], y7)
-
     for n in range(NPRE, 16):
         do_T(n)
         do_E(n)
-    y8 = stage()
-    for c in range(4):
-        emit("p", lambda: pe.matmul(T.psr[:, 64 + 8 * c:72 + 8 * c], T.aymat[:, 128 * c:128 * c + 128],
-                                    T.bymat[:, 8 * c:8 * c + 8], True, True), [y7, t_req], y8)
 
     win = T.tabT[:, 0:4096]
     nrq = {}
@@ -340,6 +321,32 @@ def rank_program(g, core, T, topo):
                 emit("v", lambda: v.tensor_copy(out, src), deps, t_g)
             emit("g", lambda: hand((kind + "0", kind + "1"), T.gout, 64, S.hr, 1), [t_g])
     t_own = one("v", lambda: v.tensor_copy(T.land[:, 64 * me:64 * me + 64], win.indirect(T.reqx[:, 4 * me:4 * me + 4])), [t_req])
+
+    y1 = one("v", lambda: v.tensor_scalar(out=T.p15i[:], in0=T.pidx[:], scalar1=15, scalar2=None, op0=A.bitwise_and), [t_pi])
+    y0 = one("v", lambda: v.tensor_scalar(out=T.sloti[:], in0=T.segf[:, 15:64:16], scalar1=0.5, scalar2=-4592.5,
+                                          op0=A.mult, op1=A.add))
+    y3 = one("v", lambda: v.tensor_tensor(out=T.rsel[:], in0=T.ident[:, 0:64], in1=T.ident[:, 64:128], op=A.add), [t_id])
+    y2 = one("v", lambda: v.tensor_scalar(out=T.p15f[:], in0=T.p15i[:], scalar1=2.0, scalar2=-31.0, op0=A.mult, op1=A.add), [y1])
+    y4 = stage()
+    emit("v", lambda: v.tensor_scalar(out=T.t16[:], in0=T.sloti[:], scalar1=16, scalar2=None, op0=A.bitwise_and), [y0], y4)
+    emit("v", lambda: v.tensor_scalar(out=T.u15[:], in0=T.sloti[:], scalar1=15, scalar2=None, op0=A.bitwise_and), (), y4)
+    y5 = stage()
+    emit("v", lambda: v.tensor_scalar(out=T.valn[:], in0=T.nf[:], scalar1=0.25, scalar2=-3328.0, op0=A.mult, op1=A.add),
+         (), y5)
+    emit("v", lambda: v.tensor_scalar(out=T.keyy[:], in0=T.t16[:], scalar1=2.0, scalar2=T.p15f[:, 0:1], op0=A.mult, op1=A.add),
+         [y4, y2], y5)
+    emit("v", lambda: v.tensor_copy(T.u15f[:], T.u15[:]), (), y5)
+    y6 = one("v", lambda: v.tensor_tensor(out=T.valy[:], in0=T.valn[:], in1=T.u15f[:], op=A.add), [y5])
+    y7 = stage()
+    for c in range(4):
+        emit("v", lambda: v.tensor_scalar(out=T.aymat[:, 128 * c:128 * c + 128], in0=T.kc2[:], scalar1=T.keyy[:, c:c + 1],
+                                          scalar2=None, op0=A.is_equal), (), y7)
+        emit("v", lambda: v.tensor_scalar(out=T.bymat[:, 8 * c:8 * c + 8], in0=T.e8[:], scalar1=T.valy[:, c:c + 1],
+                                          scalar2=None, op0=A.mult), [y6, t_e8], y7)
+    y8 = stage()
+    for c in range(4):
+        emit("p", lambda: pe.matmul(T.psr[:, 64 + 8 * c:72 + 8 * c], T.aymat[:, 128 * c:128 * c + 128],
+                                    T.bymat[:, 8 * c:8 * c + 8], True, True), [y7, t_req], y8)
     t_oy = one("v", lambda: v.tensor_scalar(out=T.offy[:], in0=T.psr[:, 64:96], scalar1=1024.0, scalar2=None, op0=A.add), [y8])
 
     t_rsp = ("rsp", sum(nrq.values()))

from concourse.bass import DstId, RemoteDMATransfer
from concourse.mybir import AluOpType, ActivationFunctionType

NCORES = 512
NPRE = 2
NSTAGE = 72


def _sb(shape, dtype="float32"):
    return ("sbuf", shape, dtype)


SCRATCH = {
    "idxs": _sb([128, 4], "int32"),
    "nat0": _sb([128, 256]), "nat1": _sb([128, 256]), "nat2": _sb([128, 512]), "nat3": _sb([128, 512]),
    "nat4": _sb([128, 256]), "nat5": _sb([128, 256]),
    "tabT": _sb([128, 4096]),
    "ident": _sb([128, 128]), "onesf": _sb([128, 128]),
    "kc2": _sb([128, 128], "bfloat16"), "nc64": _sb([128, 64], "bfloat16"), "thr64": _sb([128, 64], "bfloat16"),
    "twosb": _sb([128, 128], "bfloat16"), "lstr": _sb([128, 128], "bfloat16"), "lstr2": _sb([128, 128], "bfloat16"),
    "cstb": _sb([128, 64], "bfloat16"), "biasb": _sb([128, 64], "bfloat16"),
    "segm": _sb([128, 64]), "e8a": _sb([128, 8]), "e8": _sb([128, 8]), "rsel": _sb([128, 64]),
    "pidx": _sb([128, 1], "int32"), "p15i": _sb([128, 1], "int32"), "p15f": _sb([128, 1]),
    "ob": _sb([128, 4], "bfloat16"), "ri": _sb([128, 4], "int32"), "rowm": _sb([128, 4]),
    "hb": _sb([128, 64], "bfloat16"), "hcum": _sb([128, 192], "bfloat16"),
    "segf": _sb([128, 64]), "segb": _sb([128, 64], "bfloat16"), "nf": _sb([128, 4]),
    "sloti": _sb([128, 4], "int32"),
    "amat": _sb([128, 512], "float16"), "bmat": _sb([128, 256], "float16"),
    "reqx": _sb([128, 64], "uint16"), "offs": _sb([128, 64], "uint16"),
    "t16": _sb([128, 4], "int32"), "u15": _sb([128, 4], "int32"), "u15f": _sb([128, 4]),
    "keyy": _sb([128, 4]), "valn": _sb([128, 4]), "valy": _sb([128, 4]),
    "aymat": _sb([128, 512], "float16"), "bymat": _sb([128, 32], "float16"), "offy": _sb([128, 32], "uint16"),
    "gout": _sb([128, 1024]), "land": _sb([128, 1028]),
    "gy": _sb([128, 512]), "zz": _sb([128, 256]), "ys": _sb([128, 128]),
    "pst0": ("psum", [128, 512], "float32"), "pst1": ("psum", [128, 512], "float32"),
    "pst2": ("psum", [128, 512], "float32"), "pst3": ("psum", [128, 512], "float32"),
    "psp": ("psum", [128, 512], "float32"), "psr": ("psum", [128, 512], "float32"),
    "pso0": ("psum", [128, 512], "float32"), "pso1": ("psum", [128, 512], "float32"),
}
SEMAPHORES = (["sidx", "snat0", "snat1", "snat2", "snat3", "snat4", "snat5", "rsp", "lsem", "hq", "hr", "hl", "sy0", "sy1"]
              + ["rq%d" % r for r in range(16)] + ["x%d" % i for i in range(NSTAGE)])

_CACHE = {}
PASSED = ("far0", "far1", "rack0", "rack1", "cable0", "cable1")


def _bits(mask):
    return [i for i in range(16) if (mask >> i) & 1]


def _sub(mask, t, e):
    b = _bits(mask)
    return sum(1 << i for i in b[t::len(b) // e])


def _plan(T, topo):
    if "p" in _CACHE:
        return _CACHE["p"]
    cores = [int(x) for x in T.cores]
    groups, passer, serves, eng, pos = {}, {}, {}, {}, {}
    taken = set((topo.host(d), topo.chip(d)) for d in cores)
    for s in cores:
        gr = {"far": [], "cable": [], "rack": [], "same": []}
        for r, d in enumerate(cores):
            if d == s:
                continue
            if not topo.may_write(s, d):
                gr["far"].append(r)
            elif topo.host(d) == topo.host(s):
                gr["same"].append(r)
            elif topo.rack(topo.host(d)) == topo.rack(topo.host(s)):
                gr["rack"].append(r)
            else:
                gr["cable"].append(r)
        gr["far0"], gr["far1"] = gr["far"][0:2], gr["far"][2:4]
        groups[s] = gr
        free = [x for x in range(NCORES) if T.rank_of(x) is None and topo.chip(x) == topo.chip(s) and topo.may_write(s, x)]
        order = lambda x: (topo.die(x) != topo.die(s), x)
        near = sorted([x for x in free if topo.host(x) == topo.host(s)
                       and all(topo.may_write(x, cores[r]) for r in gr["rack"] + gr["cable"])], key=order)
        away = sorted([x for x in free if topo.rack(topo.host(x)) != topo.rack(topo.host(s))
                       and all(topo.may_write(x, cores[r]) for r in gr["far"])], key=order)
        plane = sorted([x for x in range(NCORES) if T.rank_of(x) is None and topo.same_plane(s, x) and topo.may_write(s, x)
                        and topo.host(x) != topo.host(s) and (topo.host(x), topo.chip(x)) not in taken
                        and all(topo.may_write(x, cores[r]) for r in gr["far1"])], key=order)
        taken.add((topo.host(plane[0]), topo.chip(plane[0])))
        plain = sorted([x for x in free if topo.host(x) == topo.host(s) and x not in near], key=order)
        passer[s] = {"rack0": plain[-2], "rack1": near[0], "cable0": plain[-1], "cable1": near[1],
                     "far0": away[-1], "far1": plane[0]}
        pos[s] = dict((r, r) for r in range(len(cores)))
        for k in ("rack", "cable"):
            gr[k + "0"] = [r for r in gr[k] if topo.may_write(passer[s][k + "0"], cores[r])]
            gr[k + "1"] = [r for r in gr[k] if r not in gr[k + "0"]]
            if len(gr[k + "0"]) != len(gr[k + "1"]):
                raise ValueError("uneven halves")
            for i, r in enumerate(gr[k + "0"] + gr[k + "1"]):
                pos[s][r] = gr[k][0] + i
        off = _bits(topo.mask(s, away[-1]))
        spare = [i for i in _bits(topo.mask(s, near[0])) if i not in off]
        e = len(spare) // 4
        eng[s] = {"far0": (off[0::2], off[0::2]), "far1": (off[1::2], off[1::2]),
                  "rack0": (spare[0:e], spare[0::2]), "rack1": (spare[e:2 * e], spare[1::2]),
                  "cable0": (spare[2 * e:3 * e], spare[0::2]), "cable1": (spare[3 * e:4 * e], spare[1::2])}
        for k in PASSED:
            if passer[s][k] in serves:
                raise ValueError("a passing core with two tasks")
            serves[passer[s][k]] = (s, k)
    _CACHE["p"] = {"cores": cores, "groups": groups, "passer": passer, "serves": serves, "eng": eng, "pos": pos}
    return _CACHE["p"]


def _tr(topo, src_core, dst_core, t, e, sem, src, dst):
    rid, pid = topo.addr(dst_core, src_core)
    return RemoteDMATransfer(dst_ids=[DstId(rid=rid, pnc=pid)], dma_engine_mask=_sub(topo.mask(src_core, dst_core), t, e),
                             remote_sem=sem, src=src, dst=dst)


def _share(topo, a, b, n=4):
    p = 1
    while p < n:
        p *= 2
    return len(_bits(topo.mask(a, b))) // p


def _waves(rs):
    return [rs[0:2], rs[2:3]] if len(rs) == 3 else [rs]


def _pass(g, core, s, kind, T, topo, plan):
    S, cores = T.sem, plan["cores"]
    sr = T.rank_of(s)
    tot = 0
    for ph, sem_in, sem_out, buf, land, w in ((0, S.hq, S["rq%d" % sr], T.reqx, T.offs, 4), (1, S.hr, S.rsp, T.gout, T.land, 64)):
        g.wait_ge(sem_in, len(plan["eng"][s][kind][ph]))
        trs = []
        ds = plan["groups"][s][kind]
        for t, d in enumerate(ds):
            e = _share(topo, core, cores[d], len(ds))
            a = d if ph == 0 else plan["pos"][s][d]
            b = plan["pos"][cores[d]][sr] if ph == 0 else sr
            trs.append(_tr(topo, core, cores[d], t, e, sem_out, buf[:, w * a:w * a + w], land[:, w * b:w * b + w]))
            tot += e
        g.remote_dma_fused(trs, local_sem=S.hl)
    g.wait_ge(S.hl, tot)


def rank_program(g, core, T, topo):
    plan = _plan(T, topo)
    me = T.rank_of(core)
    if me is None:
        s = plan["serves"].get(core)
        if s is not None:
            _pass(g, core, s[0], s[1], T, topo, plan)
        return
    S, cores = T.sem, plan["cores"]
    A, AF = AluOpType, ActivationFunctionType
    v, pe, sc, sy = g.vector, g.tensor, g.scalar, g.sync
    grp, passer = plan["groups"][core], plan["passer"][core]
    Q = {"v": v, "p": pe, "a": sc, "g": g, "y": sy}
    seen, nx = {}, [0]

    def stage():
        nx[0] += 1
        return ["x%d" % (nx[0] - 1), 0]

    def emit(qn, fn, deps=(), st=None):
        for d in deps:
            if d[1] > 0 and seen.get((qn, d[0]), 0) < d[1]:
                seen[(qn, d[0])] = d[1]
                Q[qn].wait_ge(S[d[0]], d[1])
        ins = fn()
        if st is not None:
            ins.then_inc(S[st[0]], 1)
            st[1] += 1
        return st

    def one(qn, fn, deps=()):
        return emit(qn, fn, deps, stage())

    pieces = [(0, 512), (512, 512), (1024, 1024), (2048, 1024), (3072, 512), (3584, 512)]
    sy.dma_start(T.idxs[:], T.idx[:]).then_inc(S.sidx, 16)
    for k, (r0, nr) in enumerate(pieces):
        (sc if k % 2 == 0 else sy).dma_start(T["nat%d" % k][:], T.tab[r0:r0 + nr, :]).then_inc(S["snat%d" % k], 16)
    t_idx = ("sidx", 16)
    blocks = [(k, u) for k, (r0, nr) in enumerate(pieces) for u in range(nr // 256)]

    t_tw = one("v", lambda: v.memset(T.twosb[:], 2.0))
    t_of = one("v", lambda: v.memset(T.onesf[:], 1.0))
    t_bi = one("v", lambda: v.memset(T.biasb[:], -31.0 / 256.0))
    t_hz = stage()
    for a, b in ((0, 16), (64, 96), (128, 176)):
        emit("v", lambda: v.memset(T.hcum[:, a:b], 0.0), (), t_hz)
    t_lz = one("v", lambda: v.memset(T.land[:, 1024:1028], 0.0))
    t_th = one("g", lambda: g.iota(T.thr64[:], [[0, 4], [4096, 16]], 786432, 0, allow_small_or_imprecise_dtypes=True))
    t_cst = one("g", lambda: g.iota(T.cstb[:], [[0, 4], [1, 16]], 0, 0, allow_small_or_imprecise_dtypes=True))
    t_l = one("g", lambda: g.affine_select(T.lstr[:], T.twosb[:], [[1, 128]], A.is_ge, 0.0, -1, -1), [t_tw])
    t_l2 = one("g", lambda: g.affine_select(T.lstr2[:], T.lstr[:], [[1, 128]], A.not_equal, 9216.0, 0, -1), [t_l])
    t_id = one("g", lambda: g.affine_select(T.ident[:], T.onesf[:], [[-1, 128]], A.is_equal, 0.0, 0, 1), [t_of])
    t_kc = one("g", lambda: g.iota(T.kc2[:], [[32, 2], [0, 4], [2, 16]], -31, 0, allow_small_or_imprecise_dtypes=True))
    t_nc = one("g", lambda: g.iota(T.nc64[:], [[64, 64]], 9216, 0, allow_small_or_imprecise_dtypes=True))
    t_e8a = one("g", lambda: g.affine_select(T.e8a[:], T.onesf[:, 0:8], [[-16, 8]], A.is_ge, 0.0, 0, 1))
    t_e8 = one("g", lambda: g.affine_select(T.e8[:], T.e8a[:], [[16, 8]], A.is_ge, 0.0, 15, -1), [t_e8a])
    t_pi = one("g", lambda: g.iota(T.pidx[:], [[0, 1]], 0, 1))
    t_sg = one("v", lambda: v.tensor_scalar(out=T.segm[:], in0=T.cstb[:], scalar1=1.0, scalar2=None, op0=A.min), [t_cst])

    tb = [stage() for b in range(4)]
    evb = [stage() for b in range(4)]

    def do_T(n):
        k, u = blocks[n]
        emit("p", lambda: pe.transpose(T["pst%d" % (n % 4)][:, 0:128], T["nat%d" % k][:, 128 * u:128 * u + 128], T.ident[:]),
             [("snat%d" % k, 16), t_id, evb[n % 4]], tb[n % 4])

    def do_E(n):
        k, u = blocks[n]
        r0, nr = pieces[k]
        qn = "v" if (n >= NPRE and n % 2 == 1) else "a"
        for h in (0, 1):
            for dup in (0, 1):
                out = T.tabT[64 * dup:64 * dup + 64, r0 + 2 * u + h:r0 + nr:nr // 128]
                in_ = T["pst%d" % (n % 4)][64 * h:64 * h + 64, 0:128]
                emit(qn, lambda: v.tensor_copy(out, in_) if qn == "v" else sc.activation(out, in_, AF.Copy),
                     [tb[n % 4]], evb[n % 4])

    s1 = one("v", lambda: v.tensor_scalar(out=T.ob[:], in0=T.idxs[:], scalar1=784384.5, scalar2=None, op0=A.add), [t_idx])
    r1 = one("v", lambda: v.tensor_scalar(out=T.ri[:], in0=T.idxs[:], scalar1=4095, scalar2=None, op0=A.bitwise_and))
    s3, s4 = stage(), stage()
    for c in range(4):
        emit("v", lambda: v.tensor_scalar(out=T.hb[:, 16 * c:16 * c + 16], in0=T.thr64[:, 0:16], scalar1=T.ob[:, c:c + 1],
                                          scalar2=None, op0=A.is_equal), [s1, t_th], s3)
    for c in range(3):
        emit("v", lambda: v.tensor_scalar(out=T.hcum[:, 64 * c + 16 * (c + 1):64 * c + 64], in0=T.thr64[:, 0:48 - 16 * c],
                                          scalar1=T.ob[:, c:c + 1], scalar2=None, op0=A.is_equal), (), s4)
    r2 = one("v", lambda: v.tensor_scalar(out=T.rowm[:], in0=T.ri[:], scalar1=-2048.0, scalar2=None, op0=A.add), [r1])
    emit("p", lambda: pe.matmul(T.psp[:, 0:64], T.twosb[:], T.cstb[:], True, False), [t_tw, t_cst])
    emit("p", lambda: pe.matmul(T.psp[:, 0:64], T.twosb[:], T.biasb[:], False, False), [t_bi])
    emit("p", lambda: pe.matmul(T.psp[:, 0:64], T.lstr2[:], T.hb[:], False, False), [t_l2, s3])
    s5 = stage()
    for c in range(3):
        emit("p", lambda: pe.matmul(T.psp[:, 0:64], T.twosb[:], T.hcum[:, 64 * c:64 * c + 64], False, c == 2), [s4, t_hz],
             s5 if c == 2 else None)
    for n in range(NPRE):
        do_T(n)
        do_E(n)
    s6 = one("v", lambda: v.tensor_tensor_scan(T.segb[:], T.segm[:], T.psp[:, 0:64], 0.0, A.mult, A.max), [s5, t_sg])
    s7 = one("v", lambda: v.tensor_tensor_scan(T.segf[:], T.segm[:], T.psp[:, 0:64], 0.0, A.mult, A.max))
    s8 = one("v", lambda: v.tensor_copy(T.nf[:], T.segb[:, 15:64:16]), [s6])
    s12 = stage()
    for c in range(4):
        s11 = stage()
        e = 16 * c + 15
        emit("v", lambda: v.tensor_scalar(out=T.amat[:, 128 * c:128 * c + 128], in0=T.kc2[:], scalar1=T.nf[:, c:c + 1],
                                          scalar2=T.segf[:, e:e + 1], op0=A.add, op1=A.is_equal), [s7, s8, t_kc], s11)
        emit("v", lambda: v.tensor_scalar(out=T.bmat[:, 64 * c:64 * c + 64], in0=T.nc64[:], scalar1=T.nf[:, c:c + 1],
                                          scalar2=T.rowm[:, c:c + 1], op0=A.is_equal, op1=A.mult), [t_nc, r2], s11)
        emit("p", lambda: pe.matmul(T.psr[:, 0:64], T.amat[:, 128 * c:128 * c + 128], T.bmat[:, 64 * c:64 * c + 64],
                                    c == 0, c == 3), [s11], s12 if c == 3 else None)
    t_req = one("v", lambda: v.tensor_scalar(out=T.reqx[:], in0=T.psr[:, 0:64], scalar1=2048.0, scalar2=None, op0=A.add), [s12])

    lsem = [0]

    def hand(kinds, buf, w, sem, ph):
        trs = []
        for kind in kinds:
            x, en = passer[kind], plan["eng"][core][kind][ph]
            if ph == 0:
                ps = grp[kind] if kind in ("far0", "far1") else grp[kind[:-1]]
            else:
                ps = sorted(plan["pos"][core][r] for r in grp[kind])
            ap = buf[:, w * ps[0]:w * ps[0] + w * len(ps)]
            rid, pid = topo.addr(x, core)
            trs.append(RemoteDMATransfer(dst_ids=[DstId(rid=rid, pnc=pid)], dma_engine_mask=sum(1 << i for i in en),
                                         remote_sem=sem, src=ap, dst=ap))
            lsem[0] += len(en)
        return g.remote_dma_fused(trs, local_sem=S.lsem)

    def fan(rs, sem, buf, w, dst):
        for wave in _waves(rs):
            trs = []
            for t, d in enumerate(wave):
                e = _share(topo, core, cores[d], len(wave))
                trs.append(_tr(topo, core, cores[d], t, e, sem, buf[:, w * d:w * d + w], dst))
                lsem[0] += e
            g.remote_dma_fused(trs, local_sem=S.lsem)

    emit("g", lambda: hand(("far0", "far1"), T.reqx, 4, S.hq, 0), [t_req])
    hand(("rack0", "rack1", "cable0", "cable1"), T.reqx, 4, S.hq, 0)
    fan(grp["same"], S["rq%d" % me], T.reqx, 4, T.offs[:, 4 * me:4 * me + 4])

    for n in range(NPRE, 16):
        do_T(n)
        do_E(n)

    win = T.tabT[:, 0:4096]
    nrq = {}
    for r, d in enumerate(cores):
        if r != me:
            last, n = d, 0
            for wave in _waves(plan["groups"][d]["same"]):
                if me in wave:
                    n = len(wave)
            for kind in PASSED:
                if me in plan["groups"][d][kind]:
                    last, n = plan["passer"][d][kind], len(plan["groups"][d][kind])
            nrq[r] = _share(topo, last, core, n)
    for kind in ("rack", "far", "cable", "same"):
        rs = grp[kind]
        deps = evb + [("rq%d" % r, nrq[r]) for r in rs]
        t_g = stage()
        if kind == "same":
            for r in rs:
                emit("a", lambda: sc.activation(T.gout[:, 64 * r:64 * r + 64], win.indirect(T.offs[:, 4 * r:4 * r + 4]), AF.Copy),
                     deps, t_g)
            emit("g", lambda: fan(rs, S.rsp, T.gout, 64, T.land[:, 64 * me:64 * me + 64]), [t_g])
        else:
            r0 = rs[0]
            out, src = T.gout[:, 64 * r0:64 * r0 + 256], win.indirect(T.offs[:, 4 * r0:4 * r0 + 16])
            if kind == "far":
                emit("a", lambda: sc.activation(out, src, AF.Copy), deps, t_g)
            else:
                emit("v", lambda: v.tensor_copy(out, src), deps, t_g)
            emit("g", lambda: hand((kind + "0", kind + "1"), T.gout, 64, S.hr, 1), [t_g])
    t_own = one("v", lambda: v.tensor_copy(T.land[:, 64 * me:64 * me + 64], win.indirect(T.reqx[:, 4 * me:4 * me + 4])), [t_req])

    y1 = one("v", lambda: v.tensor_scalar(out=T.p15i[:], in0=T.pidx[:], scalar1=15, scalar2=None, op0=A.bitwise_and), [t_pi])
    y0 = one("v", lambda: v.tensor_scalar(out=T.sloti[:], in0=T.segf[:, 15:64:16], scalar1=0.5, scalar2=-4592.5,
                                          op0=A.mult, op1=A.add))
    y3 = one("v", lambda: v.tensor_tensor(out=T.rsel[:], in0=T.ident[:, 0:64], in1=T.ident[:, 64:128], op=A.add), [t_id])
    y2 = one("v", lambda: v.tensor_scalar(out=T.p15f[:], in0=T.p15i[:], scalar1=2.0, scalar2=-31.0, op0=A.mult, op1=A.add), [y1])
    y4 = stage()
    emit("v", lambda: v.tensor_scalar(out=T.t16[:], in0=T.sloti[:], scalar1=16, scalar2=None, op0=A.bitwise_and), [y0], y4)
    emit("v", lambda: v.tensor_scalar(out=T.u15[:], in0=T.sloti[:], scalar1=15, scalar2=None, op0=A.bitwise_and), (), y4)
    y5 = stage()
    emit("v", lambda: v.tensor_scalar(out=T.valn[:], in0=T.nf[:], scalar1=0.25, scalar2=-3328.0, op0=A.mult, op1=A.add),
         (), y5)
    emit("v", lambda: v.tensor_scalar(out=T.keyy[:], in0=T.t16[:], scalar1=2.0, scalar2=T.p15f[:, 0:1], op0=A.mult, op1=A.add),
         [y4, y2], y5)
    emit("v", lambda: v.tensor_copy(T.u15f[:], T.u15[:]), (), y5)
    y6 = one("v", lambda: v.tensor_tensor(out=T.valy[:], in0=T.valn[:], in1=T.u15f[:], op=A.add), [y5])
    y7 = stage()
    for c in range(4):
        emit("v", lambda: v.tensor_scalar(out=T.aymat[:, 128 * c:128 * c + 128], in0=T.kc2[:], scalar1=T.keyy[:, c:c + 1],
                                          scalar2=None, op0=A.is_equal), (), y7)
        emit("v", lambda: v.tensor_scalar(out=T.bymat[:, 8 * c:8 * c + 8], in0=T.e8[:], scalar1=T.valy[:, c:c + 1],
                                          scalar2=None, op0=A.mult), [y6, t_e8], y7)
    y8 = stage()
    for c in range(4):
        emit("p", lambda: pe.matmul(T.psr[:, 64 + 8 * c:72 + 8 * c], T.aymat[:, 128 * c:128 * c + 128],
                                    T.bymat[:, 8 * c:8 * c + 8], True, True), [y7, t_req], y8)
    t_oy = one("v", lambda: v.tensor_scalar(out=T.offy[:], in0=T.psr[:, 64:96], scalar1=1024.0, scalar2=None, op0=A.add), [y8])

    t_rsp = ("rsp", sum(nrq.values()))
    lwin = T.land[:, 0:1028]
    ready = [t_oy, t_own, t_lz, t_rsp]
    f0 = one("v", lambda: v.tensor_copy(T.gy[:, 0:256], lwin.indirect(T.offy[:, 0:16])), ready)
    f1 = one("a", lambda: sc.activation(T.gy[:, 256:512], lwin.indirect(T.offy[:, 16:32]), AF.Copy), ready)
    z0 = one("v", lambda: v.tensor_tensor(out=T.zz[:, 0:128], in0=T.gy[:, 0:256:2], in1=T.gy[:, 1:256:2], op=A.add), [f0])
    m0 = one("p", lambda: pe.matmul(T.pso0[:, 0:64], T.zz[:, 0:128], T.rsel[:], True, True), [z0, y3])
    z1 = one("v", lambda: v.tensor_tensor(out=T.zz[:, 128:256], in0=T.gy[:, 256:512:2], in1=T.gy[:, 257:512:2], op=A.add), [f1])
    m1 = one("p", lambda: pe.matmul(T.pso1[:, 0:64], T.zz[:, 128:256], T.rsel[:], True, True), [z1])
    e0 = one("a", lambda: sc.activation(T.ys[:, 0:64], T.pso0[:, 0:64], AF.Copy), [m0])
    emit("a", lambda: sc.dma_start(T.y[0:128, :], T.ys[:, 0:64]).then_inc(S.sy0, 16), [e0])
    e1 = one("v", lambda: v.tensor_copy(T.ys[:, 64:128], T.pso1[:, 0:64]), [m1])
    emit("y", lambda: sy.dma_start(T.y[128:256, :], T.ys[:, 64:128]).then_inc(S.sy1, 16), [e1])

    emit("g", lambda: g.wait_ge(S.lsem, lsem[0]), [("sy0", 16), ("sy1", 16)])
